import numpy as np
import ml_dtypes


def mxq(x, axis, fmt="e4m3"):
    dtype, down = {"e4m3": (ml_dtypes.float8_e4m3fn, 7), "e5m2": (ml_dtypes.float8_e5m2, 14)}[fmt]
    v = np.moveaxis(np.asarray(x, np.float32).astype(ml_dtypes.bfloat16).astype(np.float64), axis, -1)
    blocks = v.reshape(v.shape[:-1] + (-1, 32))
    amax = np.abs(blocks).max(-1, keepdims=True)
    byte = np.maximum(np.where(amax > 0, np.frexp(amax)[1] - 1 + 127, 0) - down, 1)
    scale = np.exp2(byte - 127.0)
    codes = (blocks / scale).astype(np.float32).astype(dtype).astype(np.float64)
    return np.moveaxis((codes * scale).reshape(v.shape), -1, axis)


WIDE = False


def mx_kscale(k):
    if not WIDE:
        return np.ones(k)
    levels = np.array([10, -10, 5, -5, 0])
    if k % 512:
        return np.exp2(np.random.permutation(np.resize(levels, k // 32))).repeat(32)
    a = np.empty((k // 512, 16))
    for p in range(k // 512):
        a[p, :8] = np.random.permutation(np.resize(levels, 8))
        for g in range(8):
            far = levels[np.abs(levels - a[p, g]) >= 10]
            a[p, g + 8] = far[np.random.randint(len(far))]
    return np.exp2(a.ravel()).repeat(32)


BF16 = ml_dtypes.bfloat16


def bf(x):
    return np.asarray(x, np.float32).astype(BF16)


def f64(x):
    return np.asarray(x).astype(np.float64)


S, T, H, R, K = 4096, 256, 2, 2, 512
SR = S * R
TR = T * R
HS = H * S


def mix_heads(aq, ak, dot):
    aq_h = np.transpose(aq, (1, 0, 2))
    ak_h = np.transpose(ak, (1, 0, 2))
    total = 0.0
    for r in range(R):
        for j in range(R):
            left = aq_h[:, :, r][:, :, None]
            right = ak_h[:, :, j][:, None, :]
            total = total + left * right * dot[:, r, :, j][None, :, :]
    return total


def softmax_last(x):
    e = np.exp(x - np.max(x, axis=-1, keepdims=True))
    return e / np.sum(e, axis=-1, keepdims=True)


def draw0():
    s = mx_kscale(K)
    t = mx_kscale(TR).reshape(T, R)
    return {
        "bq": bf(np.random.standard_normal((S, R, K)) * s),
        "aq": bf(np.random.uniform(0.6, 1.4, (S, H, R))),
        "bk": bf(np.random.standard_normal((T, R, K)) / s),
        "ak": bf(np.random.uniform(-1.7, 1.7, (T, H, R))),
        "av": bf(np.random.uniform(-1.7, 1.7, (T, H, R)) * t[:, None, :]),
        "bv": bf(np.random.standard_normal((T, R, K)) / t[:, :, None]),
    }


def core(bq, aq, bk, ak, av, bv):
    bq2 = f64(bq).reshape(SR, K)
    bk2 = f64(bk).reshape(TR, K)
    dot = (mxq(bq2, 1, "e4m3") @ mxq(bk2, 1, "e4m3").T).reshape(S, R, T, R)

    score = (1.0 / np.sqrt(K)) * mix_heads(f64(aq), f64(ak), dot)

    p = softmax_last(score)

    av_h = np.transpose(f64(av), (1, 0, 2))
    u = p[:, :, :, None] * av_h[:, None, :, :]
    u = u.reshape(HS, TR)

    bv2 = f64(bv).reshape(TR, K)
    o = mxq(u, 1, "e4m3") @ mxq(bv2, 0, "e4m3")
    return o.reshape(H, S, K)


def e4m3fn_bytes(y):
    return np.clip(np.asarray(y, np.float64), -448.0, 448.0).astype(np.float32).astype(ml_dtypes.float8_e4m3fn).view(np.uint8)


def e4m3fn_values(b):
    return np.asarray(b, np.uint8).view(ml_dtypes.float8_e4m3fn).astype(np.float64)


def setup_inputs():
    d = draw0()
    x0 = np.asarray(d['bq']).astype(np.float64)
    s = (np.max(np.abs(x0), axis=(0, 1), keepdims=True) / 448.0).astype(np.float32)
    out = {}
    for k, v in d.items():
        if k == 'bq':
            out['bq_bytes'] = e4m3fn_bytes(x0 / s.astype(np.float64))
            out['bq_scale'] = s
        else:
            out[k] = v
    return out


def reference(bq_bytes, bq_scale, aq, bk, ak, av, bv):
    return core(e4m3fn_values(bq_bytes) * bq_scale.astype(np.float64), aq, bk, ak, av, bv)

@@ -1,0 +1,339 @@
+import math
+from contextlib import ExitStack
+
+import concourse.mybir as mybir
+from concourse.masks import make_identity
+
+S, T, H, R, K = 4096, 256, 2, 2, 512
+P = 128
+UNIT = 2 * P
+UNITS = S // UNIT
+AQ_UNITS = 4
+
+FLOPS = 2 * 2 * (S * R) * (T * R) * K
+
+F32 = mybir.dt.float32
+BF16 = mybir.dt.bfloat16
+U32 = mybir.dt.uint32
+U8 = mybir.dt.uint8
+FP8 = mybir.dt.float8_e4m3fn
+FP8X4 = mybir.dt.float8_e4m3fn_x4
+ALU = mybir.AluOpType
+ACTF = mybir.ActivationFunctionType
+AX = mybir.AxisListType
+
+
+def tile_tensorproductfactordecode_t_kernel(tc, bq_bytes, bq_scale, aq, bk, ak, av, bv, out):
+    nc = tc.nc
+    with ExitStack() as ctx:
+        keep = ctx.enter_context(tc.tile_pool(name="keep", bufs=1))
+        work = ctx.enter_context(tc.tile_pool(name="work", bufs=2))
+        psum = ctx.enter_context(tc.psum_pool(name="psum", bufs=1))
+
+        ident = keep.tile([P, P], F32, name="ident")
+        make_identity(nc, ident[:])
+
+        ctx.enter_context(tc.manual_schedule())
+
+        x_view = bq_bytes.rearrange("(n p) r k -> p n (r k)", p=P)
+        aq_view = aq.rearrange("s h r -> (s h r)")
+        x_tiles = [keep.tile([P, 2, R * K], U8, name=f"xb{u}", align_bytes=64) for u in range(UNITS)]
+        aq_tiles = [keep.tile([P, AQ_UNITS * UNIT, H, R], BF16, name=f"aq{c}") for c in range(UNITS // AQ_UNITS)]
+        sc4 = keep.tile([P, 4], F32, name="sc4")
+        ak_raw = keep.tile([P, 2 * H * R], BF16, name="ak_raw")
+        av_raw = keep.tile([P, 2 * H * R], BF16, name="av_raw")
+        bk_raw = keep.tile([P, 4, K], BF16, name="bk_raw", align_bytes=64)
+        bv_raw = keep.tile([P, 4, K], BF16, name="bv_raw", align_bytes=64)
+
+        def load_x(u):
+            nc.sync.dma_start(out=x_tiles[u][:], in_=x_view[:, 2 * u : 2 * u + 2, :])
+
+        def load_aq(c):
+            n = AQ_UNITS * UNIT * H * R
+            nc.sync.dma_start(
+                out=aq_tiles[c][:].rearrange("p s h r -> p (s h r)"),
+                in_=aq_view[c * n : (c + 1) * n].partition_broadcast(P),
+            )
+
+        load_x(0)
+        nc.scalar.dma_start(out=sc4[:], in_=bq_scale.rearrange("a b (p t) -> p (a b t)", p=P))
+        nc.scalar.dma_start(out=ak_raw[:], in_=ak.rearrange("(p tt) h j -> p (tt h j)", p=P))
+        nc.scalar.dma_start(out=av_raw[:], in_=av.rearrange("(p tt) h r -> p (tt h r)", p=P))
+        nc.sync.dma_start(out=bk_raw[:].rearrange("p x k -> p (x k)"), in_=bk.rearrange("(p tt) j k -> p (tt j k)", p=P))
+        load_x(1)
+        load_aq(0)
+        nc.sync.dma_start(out=bv_raw[:].rearrange("p x k -> p (x k)"), in_=bv.rearrange("(p tt) r k -> p (tt r k)", p=P))
+        for u in range(2, 6):
+            load_x(u)
+        load_aq(1)
+        for u in range(6, 10):
+            load_x(u)
+        load_aq(2)
+        for u in range(10, UNITS):
+            load_x(u)
+        load_aq(3)
+
+        warm = keep.tile([P, 1], F32, name="warm")
+        nc.vector.memset(warm[:], 0.0)
+        warm_out = keep.tile([P, 1], F32, name="warm_out")
+        nc.scalar.activation(warm_out[:], warm[:], ACTF.Exp)
+        ak_neg = keep.tile([P, 2, H, R], F32, name="ak_neg")
+        nc.vector.tensor_scalar(
+            ak_neg[:].rearrange("p a h j -> p (a h j)"), ak_raw[:], -1.0 / math.sqrt(K), None, op0=ALU.mult
+        )
+        av_f = keep.tile([P, H, 2, R], F32, name="av_f")
+        nc.vector.tensor_copy(av_f[:], av_raw[:].rearrange("p (a h r) -> p h a r", a=2, h=H))
+
+        kc = keep.tile([P, 4 * P], U32, name="kc", align_bytes=64)
+        ks = keep.tile([P, 4 * P], U8, name="ks", align_bytes=64)
+        vc = keep.tile([P, K], U32, name="vc", align_bytes=64)
+        vs = keep.tile([P, K], U8, name="vs", align_bytes=64)
+
+        def bank(tag, bufs, shape, dtype=F32):
+            return psum.tile(shape, dtype, name=tag, tag=tag, bufs=bufs)
+
+        def buf(tag, bufs, shape, dtype, align=64):
+            return work.tile(shape, dtype, name=tag, tag=tag, bufs=bufs, align_bytes=align)
+
+        state = {}
+
+        def prep_k():
+            kg = keep.tile([P, 4 * P, 4], BF16, name="kg", align_bytes=64)
+            kgw = kg[:].rearrange("p c t -> p (c t)").bitcast(F32).rearrange("p (c u) -> p c u", u=2)
+            words = bk_raw[:].rearrange("p x k -> p (x k)").bitcast(F32)
+            for half in range(2):
+                kt = bank("xt", 2, [P, 2, 2 * P])
+                for x2 in range(2):
+                    for u in range(2):
+                        base = (2 * half + x2) * (K // 2)
+                        nc.tensor.transpose(
+                            kt[:, u, x2 * P : (x2 + 1) * P], words[:, base + u : base + K // 2 : 2], ident[:]
+                        )
+                nc.vector.tensor_copy(
+                    out=kgw[:, half * 2 * P : (half + 1) * 2 * P, :], in_=kt[:].rearrange("p u c -> p c u")
+                )
+            nc.vector.quantize_mx(out=kc[:].bitcast(FP8X4), scales=ks[:], in_=kg[:].rearrange("p c t -> p (c t)"))
+
+        def prep_v():
+            vg = keep.tile([P, K, 4], BF16, name="vg", align_bytes=64)
+            nc.vector.tensor_copy(out=vg[:], in_=bv_raw[:].rearrange("p j n -> p n j"))
+            return vg
+
+        def prep_v_quant(vg):
+            nc.vector.quantize_mx(out=vc[:].bitcast(FP8X4), scales=vs[:], in_=vg[:].rearrange("p n t -> p (n t)"))
+
+        def cast(u, st):
+            xw = buf("xw", 4, [P, R * K], BF16)
+            nc.scalar.copy(xw[:], x_tiles[u][:, st, :].bitcast(FP8))
+            state["xw", u, st] = xw
+
+        def turn_x(u, st):
+            words = state.pop(("xw", u, st))[:].bitcast(F32)
+            xt = bank("xt", 2, [P, 2, 2 * P])
+            for r in range(R):
+                for w in range(2):
+                    base = r * (K // 2)
+                    nc.tensor.transpose(
+                        xt[:, w, r * P : (r + 1) * P], words[:, base + w : base + K // 2 : 2], ident[:]
+                    )
+            state["xt", u, st] = xt
+
+        def scale_x(u, st):
+            if st == 0:
+                state["xg", u] = buf("xg", 2, [P, 4 * P, 4], BF16)
+            xt = state.pop(("xt", u, st))
+            n = 2 * P
+            nc.vector.tensor_tensor(
+                out=state["xg", u][:, st * n : (st + 1) * n, :].rearrange("p c (w e) -> p c w e", w=2),
+                in0=xt[:].rearrange("p w c -> p (w c)").bitcast(BF16).rearrange("p (w c e) -> p c w e", w=2, e=2),
+                in1=sc4[:].rearrange("p (w e) -> p w e", w=2).unsqueeze(1).to_broadcast([P, n, 2, 2]),
+                op=ALU.mult,
+            )
+
+        def quant_x(u):
+            xg = state.pop(("xg", u))
+            xc = buf("xc", 2, [P, 4 * P], U32)
+            xs = buf("xs", 2, [P, 4 * P], U8)
+            nc.vector.quantize_mx(out=xc[:].bitcast(FP8X4), scales=xs[:], in_=xg[:].rearrange("p c t -> p (c t)"))
+            state["xq", u] = (xc, xs)
+
+        def dots(u, a):
+            xc, xs = state["xq", u]
+            for j in range(2):
+                d = bank(f"d{j}", 1, [P, 4 * P])
+                col = slice((2 * a + j) * P, (2 * a + j + 1) * P)
+                nc.tensor.matmul_mx(
+                    out=d[:], lhsT=kc[:, col].bitcast(FP8X4), lhsT_scale=ks[:, col],
+                    rhs=xc[:].bitcast(FP8X4), rhs_scale=xs[:], start=True, stop=True,
+                )
+                state["d", u, a, j] = d
+
+        def mix0(u, a, h):
+            t0 = buf("mix0", 4, [P, 4 * P], F32)
+            nc.scalar.activation(t0[:], state["d", u, a, 0][:], ACTF.Copy, scale=ak_neg[:, a, h, 0:1])
+            state["m0", u, a, h] = t0
+
+        def mix1(u, a, h):
+            f = buf("mix1", 4, [P, 4 * P], F32)
+            nc.vector.scalar_tensor_tensor(
+                out=f[:], in0=state["d", u, a, 1][:], scalar=ak_neg[:, a, h, 1:2],
+                in1=state.pop(("m0", u, a, h))[:], op0=ALU.mult, op1=ALU.add,
+            )
+            state["f", u, a, h] = f
+
+        def mixq(u, a, h):
+            g = buf("mixq", 8, [P, 2, R, P], F32)
+            q0 = (u % AQ_UNITS) * UNIT
+            nc.gpsimd.tensor_tensor(
+                out=g[:],
+                in0=state.pop(("f", u, a, h))[:].rearrange("p (st r s) -> p st r s", st=2, r=R),
+                in1=aq_tiles[u // AQ_UNITS][:, q0 : q0 + UNIT, h, :].rearrange("p (st s) r -> p st r s", st=2),
+                op=ALU.mult,
+            )
+            state["g", u, a, h] = g
+
+        def turn_scores(u, st):
+            sc = bank("sc", 1, [P, H, T])
+            for h in range(H):
+                for a in range(2):
+                    for r in range(R):
+                        nc.tensor.matmul(
+                            sc[:, h, a * P : (a + 1) * P], state["g", u, a, h][:, st, r, :], ident[:],
+                            start=(r == 0), stop=(r == R - 1), is_transpose=True,
+                        )
+            state["sc", u, st] = sc
+
+        def row_max(u, st):
+            mn = buf("mn", 3, [P, H], F32, 32)
+            nc.vector.tensor_reduce(out=mn[:], in_=state["sc", u, st][:], axis=AX.X, op=ALU.min)
+            state["mn", u, st] = mn
+
+        def expo(u, st):
+            e = buf("e", 3, [P, H, T], F32)
+            sm = buf("sm", 3, [P, H], F32, 32)
+            sc = state.pop(("sc", u, st))
+            mn = state.pop(("mn", u, st))
+            for h in range(H):
+                nc.scalar.activation(
+                    e[:, h, :], sc[:, h, :], ACTF.Exp, bias=mn[:, h : h + 1], scale=-1.0, accum_out=sm[:, h : h + 1]
+                )
+            state["e", u, st] = (e, sm)
+
+        def recip(u, st):
+            rs = buf("rs", 3, [P, H], F32, 32)
+            nc.vector.reciprocal(rs[:], state["e", u, st][1][:])
+            state["rs", u, st] = rs
+
+        def norm(u, st):
+            pn = buf("pn", 3, [P, H, T], F32)
+            e = state.pop(("e", u, st))[0]
+            rs = state.pop(("rs", u, st))
+            for h in range(H):
+                nc.gpsimd.tensor_scalar(pn[:, h, :], e[:, h, :], rs[:, h : h + 1], 0.0, op0=ALU.mult, op1=ALU.add)
+            state["pn", u, st] = pn
+
+        def turn_p(u, st):
+            pn = state.pop(("pn", u, st))
+            pt = bank("pt", 1, [P, H, 2, P])
+            for h in range(H):
+                for a in range(2):
+                    nc.tensor.transpose(pt[:, h, a, :], pn[:, h, a * P : (a + 1) * P], ident[:])
+            state["pt", u, st] = pt
+
+        def weigh(u, st, h):
+            if h == 0:
+                state["ug", u, st] = buf("ug", 3, [P, H, P, 2, R], BF16)
+            nc.vector.tensor_tensor(
+                out=state["ug", u, st][:, h],
+                in0=state["pt", u, st][:, h].rearrange("p a s -> p s a").unsqueeze(3).to_broadcast([P, P, 2, R]),
+                in1=av_f[:, h].unsqueeze(1).to_broadcast([P, P, 2, R]),
+                op=ALU.mult,
+            )
+
+        def quant_u(u, st):
+            ug = state.pop(("ug", u, st))
+            uc = buf("uc", 2, [P, H * P], U32)
+            us = buf("us", 2, [P, H * P], U8)
+            nc.vector.quantize_mx(
+                out=uc[:].bitcast(FP8X4), scales=us[:], in_=ug[:].rearrange("p h s a r -> p (h s a r)")
+            )
+            state["uq", u, st] = (uc, us)
+
+        def outs(u, st):
+            uc, us = state.pop(("uq", u, st))
+            for h in range(H):
+                o = bank("o", 2, [P, K])
+                col = slice(h * P, (h + 1) * P)
+                nc.tensor.matmul_mx(
+                    out=o[:], lhsT=uc[:, col].bitcast(FP8X4), lhsT_scale=us[:, col],
+                    rhs=vc[:].bitcast(FP8X4), rhs_scale=vs[:], start=True, stop=True,
+                )
+                state["o", u, st, h] = o
+
+        out_view = out.rearrange("h (n p) k -> n p h k", p=P)
+
+        def leave(u, st, h):
+            if h == 0:
+                state["ob", u, st] = buf("ob", 4, [P, H, K], F32)
+            ob = state["ob", u, st]
+            nc.scalar.copy(ob[:, h, :], state.pop(("o", u, st, h))[:])
+            if h == H - 1:
+                nc.sync.dma_start(out=out_view[2 * u + st], in_=ob[:])
+
+        def step(fn, u, *rest):
+            if 0 <= u < UNITS:
+                fn(u, *rest)
+
+        for i in range(-3, UNITS + 1):
+            if i == -3:
+                prep_k()
+            if i == -1:
+                vg = prep_v()
+
+            step(leave, i - 1, 0, 1)
+            step(row_max, i, 0)
+            step(expo, i, 0)
+            step(quant_u, i - 1, 1)
+            step(outs, i - 1, 1)
+            step(turn_scores, i, 1)
+            step(mix1, i + 1, 0, 0)
+            step(mix1, i + 1, 0, 1)
+            step(leave, i - 1, 1, 0)
+            step(dots, i + 1, 1)
+            step(mixq, i + 1, 0, 0)
+            step(recip, i, 0)
+            step(norm, i, 0)
+            step(mix0, i + 1, 1, 0)
+            step(leave, i - 1, 1, 1)
+            step(mix0, i + 1, 1, 1)
+            step(turn_x, i + 2, 1)
+            step(scale_x, i + 2, 0)
+            step(turn_p, i, 0)
+            step(mixq, i + 1, 0, 1)
+            step(cast, i + 3, 0)
+            step(row_max, i, 1)
+            step(expo, i, 1)
+            step(mix1, i + 1, 1, 0)
+            step(turn_x, i + 3, 0)
+            step(mix1, i + 1, 1, 1)
+            step(mixq, i + 1, 1, 0)
+            step(cast, i + 3, 1)
+            step(weigh, i, 0, 0)
+            step(recip, i, 1)
+            step(norm, i, 1)
+            step(weigh, i, 0, 1)
+            if i == -1:
+                prep_v_quant(vg)
+            step(mixq, i + 1, 1, 1)
+            step(turn_p, i, 1)
+            step(scale_x, i + 2, 1)
+            step(quant_u, i, 0)
+            step(outs, i, 0)
+            step(leave, i, 0, 0)
+            step(quant_x, i + 2)
+            step(dots, i + 2, 0)
+            step(mix0, i + 2, 0, 0)
+            step(mix0, i + 2, 0, 1)
+            step(weigh, i, 1, 0)
+            step(weigh, i, 1, 1)
+            step(turn_scores, i + 1, 0)

@@ -6,9 +6,8 @@ from concourse.masks import make_identity
 
 S, T, H, R, K = 4096, 256, 2, 2, 512
 P = 128
-UNIT = 2 * P
-UNITS = S // UNIT
-AQ_UNITS = 4
+TILES = S // P
+UNITS = TILES // 2
 
 FLOPS = 2 * 2 * (S * R) * (T * R) * K
 
@@ -21,6 +20,8 @@ FP8X4 = mybir.dt.float8_e4m3fn_x4
 ALU = mybir.AluOpType
 ACTF = mybir.ActivationFunctionType
 AX = mybir.AxisListType
+
+ON_SCALAR = ((0,1), (1,1),)
 
 
 def tile_tensorproductfactordecode_t_kernel(tc, bq_bytes, bq_scale, aq, bk, ak, av, bv, out):
@@ -35,11 +36,10 @@ def tile_tensorproductfactordecode_t_kernel(tc, bq_bytes, bq_scale, aq, bk, ak, 
 
         ctx.enter_context(tc.manual_schedule())
 
-        x_view = bq_bytes.rearrange("(n p) r k -> p n (r k)", p=P)
-        aq_view = aq.rearrange("s h r -> (s h r)")
+        x_view = bq_bytes.rearrange("(p n) r k -> p n (r k)", p=P)
         x_tiles = [keep.tile([P, 2, R * K], U8, name=f"xb{u}", align_bytes=64) for u in range(UNITS)]
-        aq_tiles = [keep.tile([P, AQ_UNITS * UNIT, H, R], BF16, name=f"aq{c}") for c in range(UNITS // AQ_UNITS)]
-        sc4 = keep.tile([P, 4], F32, name="sc4")
+        scale_row = keep.tile([P, R * K], F32, name="scale_row")
+        aq_raw = keep.tile([P, TILES * H * R], BF16, name="aq_raw")
         ak_raw = keep.tile([P, 2 * H * R], BF16, name="ak_raw")
         av_raw = keep.tile([P, 2 * H * R], BF16, name="av_raw")
         bk_raw = keep.tile([P, 4, K], BF16, name="bk_raw", align_bytes=64)
@@ -48,61 +48,53 @@ def tile_tensorproductfactordecode_t_kernel(tc, bq_bytes, bq_scale, aq, bk, ak, 
         def load_x(u):
             nc.sync.dma_start(out=x_tiles[u][:], in_=x_view[:, 2 * u : 2 * u + 2, :])
 
-        def load_aq(c):
-            n = AQ_UNITS * UNIT * H * R
-            nc.sync.dma_start(
-                out=aq_tiles[c][:].rearrange("p s h r -> p (s h r)"),
-                in_=aq_view[c * n : (c + 1) * n].partition_broadcast(P),
-            )
-
         load_x(0)
-        nc.scalar.dma_start(out=sc4[:], in_=bq_scale.rearrange("a b (p t) -> p (a b t)", p=P))
+        nc.scalar.dma_start(out=scale_row[:, 0:K], in_=bq_scale.rearrange("a b k -> (a b k)").partition_broadcast(P))
+        nc.sync.dma_start(out=bk_raw[:].rearrange("p x k -> p (x k)"), in_=bk.rearrange("(p tt) j k -> p (tt j k)", p=P))
         nc.scalar.dma_start(out=ak_raw[:], in_=ak.rearrange("(p tt) h j -> p (tt h j)", p=P))
         nc.scalar.dma_start(out=av_raw[:], in_=av.rearrange("(p tt) h r -> p (tt h r)", p=P))
-        nc.sync.dma_start(out=bk_raw[:].rearrange("p x k -> p (x k)"), in_=bk.rearrange("(p tt) j k -> p (tt j k)", p=P))
+        nc.scalar.dma_start(out=aq_raw[:], in_=aq.rearrange("(p n) h r -> p (n h r)", p=P))
         load_x(1)
-        load_aq(0)
         nc.sync.dma_start(out=bv_raw[:].rearrange("p x k -> p (x k)"), in_=bv.rearrange("(p tt) r k -> p (tt r k)", p=P))
-        for u in range(2, 6):
+        for u in range(2, UNITS):
             load_x(u)
-        load_aq(1)
-        for u in range(6, 10):
-            load_x(u)
-        load_aq(2)
-        for u in range(10, UNITS):
-            load_x(u)
-        load_aq(3)
 
         warm = keep.tile([P, 1], F32, name="warm")
         nc.vector.memset(warm[:], 0.0)
         warm_out = keep.tile([P, 1], F32, name="warm_out")
         nc.scalar.activation(warm_out[:], warm[:], ACTF.Exp)
-        ak_neg = keep.tile([P, 2, H, R], F32, name="ak_neg")
-        nc.vector.tensor_scalar(
-            ak_neg[:].rearrange("p a h j -> p (a h j)"), ak_raw[:], -1.0 / math.sqrt(K), None, op0=ALU.mult
-        )
+        nc.vector.tensor_copy(scale_row[:, K : R * K], scale_row[:, 0:K])
+        ak_f = keep.tile([P, 2, H, R], F32, name="ak_f")
+        nc.vector.tensor_copy(ak_f[:].rearrange("p a h j -> p (a h j)"), ak_raw[:])
         av_f = keep.tile([P, H, 2, R], F32, name="av_f")
         nc.vector.tensor_copy(av_f[:], av_raw[:].rearrange("p (a h r) -> p h a r", a=2, h=H))
+        aq_neg = keep.tile([P, TILES, H, R], F32, name="aq_neg")
+        nc.vector.tensor_scalar(
+            aq_neg[:].rearrange("p n h r -> p (n h r)"), aq_raw[:], -1.0 / math.sqrt(K), None, op0=ALU.mult
+        )
 
         kc = keep.tile([P, 4 * P], U32, name="kc", align_bytes=64)
         ks = keep.tile([P, 4 * P], U8, name="ks", align_bytes=64)
         vc = keep.tile([P, K], U32, name="vc", align_bytes=64)
         vs = keep.tile([P, K], U8, name="vs", align_bytes=64)
 
-        def bank(tag, bufs, shape, dtype=F32):
-            return psum.tile(shape, dtype, name=tag, tag=tag, bufs=bufs)
+        def bank(tag, shape, bufs=1):
+            return psum.tile(shape, F32, name=tag, tag=tag, bufs=bufs)
 
         def buf(tag, bufs, shape, dtype, align=64):
             return work.tile(shape, dtype, name=tag, tag=tag, bufs=bufs, align_bytes=align)
 
         state = {}
 
+        def words_of(tile_ap):
+            return tile_ap.bitcast(F32).rearrange("p (c u) -> p c u", u=2)
+
         def prep_k():
             kg = keep.tile([P, 4 * P, 4], BF16, name="kg", align_bytes=64)
-            kgw = kg[:].rearrange("p c t -> p (c t)").bitcast(F32).rearrange("p (c u) -> p c u", u=2)
+            kgw = words_of(kg[:].rearrange("p c t -> p (c t)"))
             words = bk_raw[:].rearrange("p x k -> p (x k)").bitcast(F32)
             for half in range(2):
-                kt = bank("xt", 2, [P, 2, 2 * P])
+                kt = bank("xt", [P, 2, 2 * P], 1)
                 for x2 in range(2):
                     for u in range(2):
                         base = (2 * half + x2) * (K // 2)
@@ -114,22 +106,27 @@ def tile_tensorproductfactordecode_t_kernel(tc, bq_bytes, bq_scale, aq, bk, ak, 
                 )
             nc.vector.quantize_mx(out=kc[:].bitcast(FP8X4), scales=ks[:], in_=kg[:].rearrange("p c t -> p (c t)"))
 
-        def prep_v():
-            vg = keep.tile([P, K, 4], BF16, name="vg", align_bytes=64)
-            nc.vector.tensor_copy(out=vg[:], in_=bv_raw[:].rearrange("p j n -> p n j"))
-            return vg
+        vg = keep.tile([P, K, 4], BF16, name="vg", align_bytes=64)
 
-        def prep_v_quant(vg):
+        def prep_v():
+            nc.vector.tensor_copy(out=vg[:], in_=bv_raw[:].rearrange("p j n -> p n j"))
+
+        def prep_v_quant():
             nc.vector.quantize_mx(out=vc[:].bitcast(FP8X4), scales=vs[:], in_=vg[:].rearrange("p n t -> p (n t)"))
 
         def cast(u, st):
             xw = buf("xw", 4, [P, R * K], BF16)
-            nc.scalar.copy(xw[:], x_tiles[u][:, st, :].bitcast(FP8))
+            nc.vector.tensor_tensor(
+                out=xw[:],
+                in0=x_tiles[u][:, st, :].bitcast(FP8),
+                in1=scale_row[:],
+                op=ALU.mult,
+            )
             state["xw", u, st] = xw
 
         def turn_x(u, st):
             words = state.pop(("xw", u, st))[:].bitcast(F32)
-            xt = bank("xt", 2, [P, 2, 2 * P])
+            xt = bank("xt", [P, 2, 2 * P], 1)
             for r in range(R):
                 for w in range(2):
                     base = r * (K // 2)
@@ -138,16 +135,14 @@ def tile_tensorproductfactordecode_t_kernel(tc, bq_bytes, bq_scale, aq, bk, ak, 
                     )
             state["xt", u, st] = xt
 
-        def scale_x(u, st):
-            if st == 0:
+        def gather_x(u, st):
+            if ("xg", u) not in state:
                 state["xg", u] = buf("xg", 2, [P, 4 * P, 4], BF16)
             xt = state.pop(("xt", u, st))
             n = 2 * P
-            nc.vector.tensor_tensor(
-                out=state["xg", u][:, st * n : (st + 1) * n, :].rearrange("p c (w e) -> p c w e", w=2),
-                in0=xt[:].rearrange("p w c -> p (w c)").bitcast(BF16).rearrange("p (w c e) -> p c w e", w=2, e=2),
-                in1=sc4[:].rearrange("p (w e) -> p w e", w=2).unsqueeze(1).to_broadcast([P, n, 2, 2]),
-                op=ALU.mult,
+            nc.scalar.copy(
+                words_of(state["xg", u][:].rearrange("p c t -> p (c t)"))[:, st * n : (st + 1) * n, :],
+                xt[:].rearrange("p w c -> p c w"),
             )
 
         def quant_x(u):
@@ -160,7 +155,7 @@ def tile_tensorproductfactordecode_t_kernel(tc, bq_bytes, bq_scale, aq, bk, ak, 
         def dots(u, a):
             xc, xs = state["xq", u]
             for j in range(2):
-                d = bank(f"d{j}", 1, [P, 4 * P])
+                d = bank(f"d{j}", [P, 4 * P])
                 col = slice((2 * a + j) * P, (2 * a + j + 1) * P)
                 nc.tensor.matmul_mx(
                     out=d[:], lhsT=kc[:, col].bitcast(FP8X4), lhsT_scale=ks[:, col],
@@ -169,53 +164,68 @@ def tile_tensorproductfactordecode_t_kernel(tc, bq_bytes, bq_scale, aq, bk, ak, 
                 state["d", u, a, j] = d
 
         def mix0(u, a, h):
-            t0 = buf("mix0", 4, [P, 4 * P], F32)
-            nc.scalar.activation(t0[:], state["d", u, a, 0][:], ACTF.Copy, scale=ak_neg[:, a, h, 0:1])
+            t0 = buf("mix0", 10, [P, 4 * P], F32)
+            nc.scalar.activation(t0[:], state["d", u, a, 0][:], ACTF.Copy, scale=ak_f[:, a, h, 0:1])
             state["m0", u, a, h] = t0
 
         def mix1(u, a, h):
-            f = buf("mix1", 4, [P, 4 * P], F32)
-            nc.vector.scalar_tensor_tensor(
-                out=f[:], in0=state["d", u, a, 1][:], scalar=ak_neg[:, a, h, 1:2],
-                in1=state.pop(("m0", u, a, h))[:], op0=ALU.mult, op1=ALU.add,
-            )
-            state["f", u, a, h] = f
+            f = buf("mix1", 10, [P, 4 * P], F32)
+            if (a, h) in ON_SCALAR:
+                nc.scalar.activation(f[:], state["d", u, a, 1][:], ACTF.Copy, scale=ak_f[:, a, h, 1:2])
+            else:
+                nc.vector.scalar_tensor_tensor(
+                    out=f[:], in0=state["d", u, a, 1][:], scalar=ak_f[:, a, h, 1:2],
+                    in1=state["m0", u, a, h][:], op0=ALU.mult, op1=ALU.add,
+                )
+            state["m1", u, a, h] = f
 
-        def mixq(u, a, h):
-            g = buf("mixq", 8, [P, 2, R, P], F32)
-            q0 = (u % AQ_UNITS) * UNIT
-            nc.gpsimd.tensor_tensor(
-                out=g[:],
-                in0=state.pop(("f", u, a, h))[:].rearrange("p (st r s) -> p st r s", st=2, r=R),
-                in1=aq_tiles[u // AQ_UNITS][:, q0 : q0 + UNIT, h, :].rearrange("p (st s) r -> p st r s", st=2),
-                op=ALU.mult,
-            )
-            state["g", u, a, h] = g
-
-        def turn_scores(u, st):
-            sc = bank("sc", 1, [P, H, T])
-            for h in range(H):
+        def turn_f(u, st):
+            for r in range(R):
+                s = bank(f"s{r}", [P, H, T])
                 for a in range(2):
-                    for r in range(R):
-                        nc.tensor.matmul(
-                            sc[:, h, a * P : (a + 1) * P], state["g", u, a, h][:, st, r, :], ident[:],
-                            start=(r == 0), stop=(r == R - 1), is_transpose=True,
-                        )
-            state["sc", u, st] = sc
+                    for h in range(H):
+                        parts = [state["m1", u, a, h]]
+                        if (a, h) in ON_SCALAR:
+                            parts.append(state["m0", u, a, h])
+                        col = slice((st * R + r) * P, (st * R + r + 1) * P)
+                        for n, part in enumerate(parts):
+                            nc.tensor.matmul(
+                                s[:, h, a * P : (a + 1) * P], part[:, col], ident[:],
+                                start=(n == 0), stop=(n == len(parts) - 1), is_transpose=True,
+                            )
+                state["s", u, st, r] = s
+
+        def rank0(u, st):
+            s = state.pop(("s", u, st, 0))
+            b0 = buf("b0", 3, [P, H, T], F32)
+            for h in range(H):
+                nc.scalar.activation(b0[:, h, :], s[:, h, :], ACTF.Copy, scale=aq_neg[:, 2 * u + st, h, 0:1])
+            state["b0", u, st] = b0
+
+        def rank1(u, st):
+            s = state.pop(("s", u, st, 1))
+            b0 = state.pop(("b0", u, st))
+            b = buf("b", 3, [P, H, T], F32)
+            for h in range(H):
+                nc.vector.scalar_tensor_tensor(
+                    out=b[:, h, :], in0=s[:, h, :], scalar=aq_neg[:, 2 * u + st, h, 1:2], in1=b0[:, h, :],
+                    op0=ALU.mult, op1=ALU.add,
+                )
+            state["b", u, st] = b
 
         def row_max(u, st):
             mn = buf("mn", 3, [P, H], F32, 32)
-            nc.vector.tensor_reduce(out=mn[:], in_=state["sc", u, st][:], axis=AX.X, op=ALU.min)
+            nc.vector.tensor_reduce(out=mn[:], in_=state["b", u, st][:], axis=AX.X, op=ALU.min)
             state["mn", u, st] = mn
 
         def expo(u, st):
             e = buf("e", 3, [P, H, T], F32)
             sm = buf("sm", 3, [P, H], F32, 32)
-            sc = state.pop(("sc", u, st))
+            b = state.pop(("b", u, st))
             mn = state.pop(("mn", u, st))
             for h in range(H):
                 nc.scalar.activation(
-                    e[:, h, :], sc[:, h, :], ACTF.Exp, bias=mn[:, h : h + 1], scale=-1.0, accum_out=sm[:, h : h + 1]
+                    e[:, h, :], b[:, h, :], ACTF.Exp, bias=mn[:, h : h + 1], scale=-1.0, accum_out=sm[:, h : h + 1]
                 )
             state["e", u, st] = (e, sm)
 
@@ -229,19 +239,19 @@ def tile_tensorproductfactordecode_t_kernel(tc, bq_bytes, bq_scale, aq, bk, ak, 
             e = state.pop(("e", u, st))[0]
             rs = state.pop(("rs", u, st))
             for h in range(H):
-                nc.gpsimd.tensor_scalar(pn[:, h, :], e[:, h, :], rs[:, h : h + 1], 0.0, op0=ALU.mult, op1=ALU.add)
+                nc.vector.tensor_scalar(pn[:, h, :], e[:, h, :], rs[:, h : h + 1], None, op0=ALU.mult)
             state["pn", u, st] = pn
 
         def turn_p(u, st):
             pn = state.pop(("pn", u, st))
-            pt = bank("pt", 1, [P, H, 2, P])
+            pt = bank("pt", [P, H, 2, P])
             for h in range(H):
                 for a in range(2):
                     nc.tensor.transpose(pt[:, h, a, :], pn[:, h, a * P : (a + 1) * P], ident[:])
             state["pt", u, st] = pt
 
         def weigh(u, st, h):
-            if h == 0:
+            if ("ug", u, st) not in state:
                 state["ug", u, st] = buf("ug", 3, [P, H, P, 2, R], BF16)
             nc.vector.tensor_tensor(
                 out=state["ug", u, st][:, h],
@@ -252,8 +262,8 @@ def tile_tensorproductfactordecode_t_kernel(tc, bq_bytes, bq_scale, aq, bk, ak, 
 
         def quant_u(u, st):
             ug = state.pop(("ug", u, st))
-            uc = buf("uc", 2, [P, H * P], U32)
-            us = buf("us", 2, [P, H * P], U8)
+            uc = buf("uc", 3, [P, H * P], U32)
+            us = buf("us", 3, [P, H * P], U8)
             nc.vector.quantize_mx(
                 out=uc[:].bitcast(FP8X4), scales=us[:], in_=ug[:].rearrange("p h s a r -> p (h s a r)")
             )
@@ -262,7 +272,7 @@ def tile_tensorproductfactordecode_t_kernel(tc, bq_bytes, bq_scale, aq, bk, ak, 
         def outs(u, st):
             uc, us = state.pop(("uq", u, st))
             for h in range(H):
-                o = bank("o", 2, [P, K])
+                o = bank("o", [P, K], 2)
                 col = slice(h * P, (h + 1) * P)
                 nc.tensor.matmul_mx(
                     out=o[:], lhsT=uc[:, col].bitcast(FP8X4), lhsT_scale=us[:, col],
@@ -270,70 +280,71 @@ def tile_tensorproductfactordecode_t_kernel(tc, bq_bytes, bq_scale, aq, bk, ak, 
                 )
                 state["o", u, st, h] = o
 
-        out_view = out.rearrange("h (n p) k -> n p h k", p=P)
+        out_view = out.rearrange("h (p n) k -> n p h k", p=P)
 
         def leave(u, st, h):
-            if h == 0:
+            if ("ob", u, st) not in state:
                 state["ob", u, st] = buf("ob", 4, [P, H, K], F32)
+                state["left", u, st] = 0
             ob = state["ob", u, st]
             nc.scalar.copy(ob[:, h, :], state.pop(("o", u, st, h))[:])
-            if h == H - 1:
+            state["left", u, st] += 1
+            if state["left", u, st] == H:
                 nc.sync.dma_start(out=out_view[2 * u + st], in_=ob[:])
 
         def step(fn, u, *rest):
             if 0 <= u < UNITS:
                 fn(u, *rest)
 
-        for i in range(-3, UNITS + 1):
-            if i == -3:
+        for i in range(-4, UNITS - (-1)):
+            if i == -4:
                 prep_k()
             if i == -1:
-                vg = prep_v()
-
+                prep_v()
+            if i == 0:
+                prep_v_quant()
             step(leave, i - 1, 0, 1)
-            step(row_max, i, 0)
-            step(expo, i, 0)
-            step(quant_u, i - 1, 1)
-            step(outs, i - 1, 1)
-            step(turn_scores, i, 1)
-            step(mix1, i + 1, 0, 0)
-            step(mix1, i + 1, 0, 1)
-            step(leave, i - 1, 1, 0)
-            step(dots, i + 1, 1)
-            step(mixq, i + 1, 0, 0)
+            step(weigh, i - 1, 1, 0)
             step(recip, i, 0)
+            step(rank0, i, 1)
+            step(quant_u, i - 1, 1)
             step(norm, i, 0)
-            step(mix0, i + 1, 1, 0)
-            step(leave, i - 1, 1, 1)
-            step(mix0, i + 1, 1, 1)
-            step(turn_x, i + 2, 1)
-            step(scale_x, i + 2, 0)
-            step(turn_p, i, 0)
-            step(mixq, i + 1, 0, 1)
-            step(cast, i + 3, 0)
-            step(row_max, i, 1)
-            step(expo, i, 1)
-            step(mix1, i + 1, 1, 0)
-            step(turn_x, i + 3, 0)
-            step(mix1, i + 1, 1, 1)
-            step(mixq, i + 1, 1, 0)
+            step(rank1, i, 1)
+            step(mix1, i + 1, 0, 1)
+            step(outs, i - 1, 1)
+            step(gather_x, i + 2, 1)
+            step(dots, i + 1, 1)
             step(cast, i + 3, 1)
-            step(weigh, i, 0, 0)
-            step(recip, i, 1)
-            step(norm, i, 1)
+            step(leave, i - 1, 1, 1)
+            step(turn_p, i, 0)
+            step(turn_x, i + 3, 0)
+            step(row_max, i, 1)
             step(weigh, i, 0, 1)
-            if i == -1:
-                prep_v_quant(vg)
-            step(mixq, i + 1, 1, 1)
-            step(turn_p, i, 1)
-            step(scale_x, i + 2, 1)
+            step(mix0, i + 1, 1, 0)
+            step(mix1, i + 1, 1, 1)
+            step(mix0, i + 1, 1, 1)
+            step(leave, i - 1, 1, 0)
+            step(expo, i, 1)
+            step(gather_x, i + 3, 0)
+            step(mix1, i + 1, 1, 0)
+            step(turn_f, i + 1, 0)
+            step(weigh, i, 0, 0)
+            step(quant_x, i + 2)
+            step(rank0, i + 1, 0)
             step(quant_u, i, 0)
             step(outs, i, 0)
             step(leave, i, 0, 0)
-            step(quant_x, i + 2)
             step(dots, i + 2, 0)
+            step(cast, i + 4, 0)
             step(mix0, i + 2, 0, 0)
+            step(recip, i, 1)
+            step(rank1, i + 1, 0)
+            step(norm, i, 1)
             step(mix0, i + 2, 0, 1)
-            step(weigh, i, 1, 0)
+            step(turn_p, i, 1)
+            step(row_max, i + 1, 0)
+            step(mix1, i + 2, 0, 0)
+            step(turn_f, i + 1, 1)
             step(weigh, i, 1, 1)
-            step(turn_scores, i + 1, 0)
+            step(expo, i + 1, 0)
+            step(turn_x, i + 3, 1)

@@ -8,6 +8,8 @@ S, T, H, R, K = 4096, 256, 2, 2, 512
 P = 128
 TILES = S // P
 UNITS = TILES // 2
+UNIT = 2 * P
+AQ_UNITS = 2
 
 FLOPS = 2 * 2 * (S * R) * (T * R) * K
 
@@ -20,8 +22,6 @@ FP8X4 = mybir.dt.float8_e4m3fn_x4
 ALU = mybir.AluOpType
 ACTF = mybir.ActivationFunctionType
 AX = mybir.AxisListType
-
-ON_SCALAR = ((0,1), (1,1),)
 
 
 def tile_tensorproductfactordecode_t_kernel(tc, bq_bytes, bq_scale, aq, bk, ak, av, bv, out):
@@ -36,49 +36,65 @@ def tile_tensorproductfactordecode_t_kernel(tc, bq_bytes, bq_scale, aq, bk, ak, 
 
         ctx.enter_context(tc.manual_schedule())
 
-        x_view = bq_bytes.rearrange("(p n) r k -> p n (r k)", p=P)
-        x_tiles = [keep.tile([P, 2, R * K], U8, name=f"xb{u}", align_bytes=64) for u in range(UNITS)]
-        scale_row = keep.tile([P, R * K], F32, name="scale_row")
-        aq_raw = keep.tile([P, TILES * H * R], BF16, name="aq_raw")
+        x_view = bq_bytes.rearrange("(n p) r k -> p n (r k)", p=P)
+        x_tiles = [keep.tile([P, 2 * R * K], U8, name=f"xb{u}", align_bytes=64) for u in range(UNITS)]
+        scale_row = keep.tile([P, 2 * R * K], F32, name="scale_row")
+        aq_cols = [keep.tile([P, AQ_UNITS * UNIT, H, R], BF16, name=f"aqc{c}") for c in range(UNITS // AQ_UNITS)]
+        aq_raw = keep.tile([P, TILES, H * R], BF16, name="aq_raw")
         ak_raw = keep.tile([P, 2 * H * R], BF16, name="ak_raw")
         av_raw = keep.tile([P, 2 * H * R], BF16, name="av_raw")
         bk_raw = keep.tile([P, 4, K], BF16, name="bk_raw", align_bytes=64)
         bv_raw = keep.tile([P, 4, K], BF16, name="bv_raw", align_bytes=64)
 
         def load_x(u):
-            nc.sync.dma_start(out=x_tiles[u][:], in_=x_view[:, 2 * u : 2 * u + 2, :])
+            nc.sync.dma_start(
+                out=x_tiles[u][:].rearrange("p (n c) -> p n c", n=2), in_=x_view[:, 2 * u : 2 * u + 2, :]
+            )
+
+        aq_flat = aq.rearrange("s h r -> (s h r)")
+
+        def load_aq(c):
+            n = AQ_UNITS * UNIT * H * R
+            nc.sync.dma_start(
+                out=aq_cols[c][:].rearrange("p s h r -> p (s h r)"),
+                in_=aq_flat[c * n : (c + 1) * n].partition_broadcast(P),
+            )
 
         load_x(0)
         nc.scalar.dma_start(out=scale_row[:, 0:K], in_=bq_scale.rearrange("a b k -> (a b k)").partition_broadcast(P))
         nc.sync.dma_start(out=bk_raw[:].rearrange("p x k -> p (x k)"), in_=bk.rearrange("(p tt) j k -> p (tt j k)", p=P))
         nc.scalar.dma_start(out=ak_raw[:], in_=ak.rearrange("(p tt) h j -> p (tt h j)", p=P))
         nc.scalar.dma_start(out=av_raw[:], in_=av.rearrange("(p tt) h r -> p (tt h r)", p=P))
-        nc.scalar.dma_start(out=aq_raw[:], in_=aq.rearrange("(p n) h r -> p (n h r)", p=P))
+        load_aq(0)
         load_x(1)
+        nc.sync.dma_start(out=aq_raw[:], in_=aq.rearrange("(n p) h r -> p n (h r)", p=P))
         nc.sync.dma_start(out=bv_raw[:].rearrange("p x k -> p (x k)"), in_=bv.rearrange("(p tt) r k -> p (tt r k)", p=P))
         for u in range(2, UNITS):
             load_x(u)
+            if u % 2 == 0:
+                load_aq(u // 2)
 
         warm = keep.tile([P, 1], F32, name="warm")
         nc.vector.memset(warm[:], 0.0)
         warm_out = keep.tile([P, 1], F32, name="warm_out")
         nc.scalar.activation(warm_out[:], warm[:], ACTF.Exp)
-        nc.vector.tensor_copy(scale_row[:, K : R * K], scale_row[:, 0:K])
-        ak_f = keep.tile([P, 2, H, R], F32, name="ak_f")
-        nc.vector.tensor_copy(ak_f[:].rearrange("p a h j -> p (a h j)"), ak_raw[:])
-        av_f = keep.tile([P, H, 2, R], F32, name="av_f")
-        nc.vector.tensor_copy(av_f[:], av_raw[:].rearrange("p (a h r) -> p h a r", a=2, h=H))
-        aq_neg = keep.tile([P, TILES, H, R], F32, name="aq_neg")
-        nc.vector.tensor_scalar(
-            aq_neg[:].rearrange("p n h r -> p (n h r)"), aq_raw[:], -1.0 / math.sqrt(K), None, op0=ALU.mult
+        nc.vector.tensor_copy(scale_row[:, K : 2 * K], scale_row[:, 0:K])
+        nc.vector.tensor_copy(scale_row[:, 2 * K : 4 * K], scale_row[:, 0 : 2 * K])
+        ak_neg = keep.tile([P, 2, H, R], F32, name="ak_neg")
+        nc.gpsimd.tensor_scalar(
+            ak_neg[:].rearrange("p a h j -> p (a h j)"), ak_raw[:], -1.0 / math.sqrt(K), 0.0, op0=ALU.mult, op1=ALU.add
         )
+        av_f = keep.tile([P, H, 2, R], F32, name="av_f")
+        nc.gpsimd.tensor_copy(av_f[:], av_raw[:].rearrange("p (a h r) -> p h a r", a=2, h=H))
+        aq_f = keep.tile([P, TILES, H, R], F32, name="aq_f")
+        nc.gpsimd.tensor_copy(out=aq_f[:].rearrange("p n h r -> p (n h r)"), in_=aq_raw[:].rearrange("p n c -> p (n c)"))
 
         kc = keep.tile([P, 4 * P], U32, name="kc", align_bytes=64)
         ks = keep.tile([P, 4 * P], U8, name="ks", align_bytes=64)
         vc = keep.tile([P, K], U32, name="vc", align_bytes=64)
         vs = keep.tile([P, K], U8, name="vs", align_bytes=64)
 
-        def bank(tag, shape, bufs=1):
+        def bank(tag, shape, bufs):
             return psum.tile(shape, F32, name=tag, tag=tag, bufs=bufs)
 
         def buf(tag, bufs, shape, dtype, align=64):
@@ -101,35 +117,33 @@ def tile_tensorproductfactordecode_t_kernel(tc, bq_bytes, bq_scale, aq, bk, ak, 
                         nc.tensor.transpose(
                             kt[:, u, x2 * P : (x2 + 1) * P], words[:, base + u : base + K // 2 : 2], ident[:]
                         )
-                nc.vector.tensor_copy(
+                nc.scalar.copy(
                     out=kgw[:, half * 2 * P : (half + 1) * 2 * P, :], in_=kt[:].rearrange("p u c -> p c u")
                 )
+            return kg
+
+        def prep_k_quant(kg):
             nc.vector.quantize_mx(out=kc[:].bitcast(FP8X4), scales=ks[:], in_=kg[:].rearrange("p c t -> p (c t)"))
 
         vg = keep.tile([P, K, 4], BF16, name="vg", align_bytes=64)
 
         def prep_v():
-            nc.vector.tensor_copy(out=vg[:], in_=bv_raw[:].rearrange("p j n -> p n j"))
+            nc.scalar.copy(out=vg[:], in_=bv_raw[:].rearrange("p j n -> p n j"))
 
         def prep_v_quant():
             nc.vector.quantize_mx(out=vc[:].bitcast(FP8X4), scales=vs[:], in_=vg[:].rearrange("p n t -> p (n t)"))
 
-        def cast(u, st):
-            xw = buf("xw", 4, [P, R * K], BF16)
-            nc.vector.tensor_tensor(
-                out=xw[:],
-                in0=x_tiles[u][:, st, :].bitcast(FP8),
-                in1=scale_row[:],
-                op=ALU.mult,
-            )
-            state["xw", u, st] = xw
+        def cast(u):
+            xw = buf("xw", 4, [P, 2 * R * K], BF16)
+            nc.vector.tensor_tensor(out=xw[:], in0=x_tiles[u][:].bitcast(FP8), in1=scale_row[:], op=ALU.mult)
+            state["xw", u] = xw
 
         def turn_x(u, st):
-            words = state.pop(("xw", u, st))[:].bitcast(F32)
-            xt = bank("xt", [P, 2, 2 * P], 1)
+            words = state["xw", u][:].bitcast(F32)
+            xt = bank("xt", [P, 2, R * P], 1)
             for r in range(R):
                 for w in range(2):
-                    base = r * (K // 2)
+                    base = (st * R + r) * (K // 2)
                     nc.tensor.transpose(
                         xt[:, w, r * P : (r + 1) * P], words[:, base + w : base + K // 2 : 2], ident[:]
                     )
@@ -137,25 +151,22 @@ def tile_tensorproductfactordecode_t_kernel(tc, bq_bytes, bq_scale, aq, bk, ak, 
 
         def gather_x(u, st):
             if ("xg", u) not in state:
-                state["xg", u] = buf("xg", 2, [P, 4 * P, 4], BF16)
+                state["xg", u] = buf("xg", 2, [P, R * 2 * P * 4], BF16)
             xt = state.pop(("xt", u, st))
-            n = 2 * P
-            nc.scalar.copy(
-                words_of(state["xg", u][:].rearrange("p c t -> p (c t)"))[:, st * n : (st + 1) * n, :],
-                xt[:].rearrange("p w c -> p c w"),
-            )
+            xgw = state["xg", u][:].bitcast(F32).rearrange("p (r n s w) -> p r n s w", r=R, n=2, w=2)
+            nc.scalar.copy(xgw[:, :, st, :, :], xt[:].rearrange("p w (r s) -> p r s w", r=R))
 
         def quant_x(u):
             xg = state.pop(("xg", u))
             xc = buf("xc", 2, [P, 4 * P], U32)
             xs = buf("xs", 2, [P, 4 * P], U8)
-            nc.vector.quantize_mx(out=xc[:].bitcast(FP8X4), scales=xs[:], in_=xg[:].rearrange("p c t -> p (c t)"))
+            nc.vector.quantize_mx(out=xc[:].bitcast(FP8X4), scales=xs[:], in_=xg[:])
             state["xq", u] = (xc, xs)
 
         def dots(u, a):
             xc, xs = state["xq", u]
             for j in range(2):
-                d = bank(f"d{j}", [P, 4 * P])
+                d = bank(f"d{j}", [P, 4 * P], 1)
                 col = slice((2 * a + j) * P, (2 * a + j + 1) * P)
                 nc.tensor.matmul_mx(
                     out=d[:], lhsT=kc[:, col].bitcast(FP8X4), lhsT_scale=ks[:, col],
@@ -163,188 +174,192 @@ def tile_tensorproductfactordecode_t_kernel(tc, bq_bytes, bq_scale, aq, bk, ak, 
                 )
                 state["d", u, a, j] = d
 
-        def mix0(u, a, h):
-            t0 = buf("mix0", 10, [P, 4 * P], F32)
-            nc.scalar.activation(t0[:], state["d", u, a, 0][:], ACTF.Copy, scale=ak_f[:, a, h, 0:1])
-            state["m0", u, a, h] = t0
+        def in_full(u, h):
+            return h == 0
 
-        def mix1(u, a, h):
-            f = buf("mix1", 10, [P, 4 * P], F32)
-            if (a, h) in ON_SCALAR:
-                nc.scalar.activation(f[:], state["d", u, a, 1][:], ACTF.Copy, scale=ak_f[:, a, h, 1:2])
-            else:
+        def mix(u, a, j, h):
+            m = buf(f"mix{h}", 10, [P, R * UNIT], F32)
+            d = state["d", u, a, j]
+            if in_full(u, h):
+                q0 = (u % AQ_UNITS) * UNIT
                 nc.vector.scalar_tensor_tensor(
-                    out=f[:], in0=state["d", u, a, 1][:], scalar=ak_f[:, a, h, 1:2],
-                    in1=state["m0", u, a, h][:], op0=ALU.mult, op1=ALU.add,
+                    out=m[:].rearrange("p (r c) -> p r c", r=R),
+                    in0=d[:].rearrange("p (r c) -> p r c", r=R),
+                    scalar=ak_neg[:, a, h, j : j + 1],
+                    in1=aq_cols[u // AQ_UNITS][:, q0 : q0 + UNIT, h, :].rearrange("p c r -> p r c"),
+                    op0=ALU.mult, op1=ALU.mult,
                 )
-            state["m1", u, a, h] = f
+            else:
+                nc.scalar.activation(m[:], d[:], ACTF.Copy, scale=ak_neg[:, a, h, j : j + 1])
+            state["m", u, a, j, h] = m
 
-        def turn_f(u, st):
-            for r in range(R):
-                s = bank(f"s{r}", [P, H, T])
-                for a in range(2):
-                    for h in range(H):
-                        parts = [state["m1", u, a, h]]
-                        if (a, h) in ON_SCALAR:
-                            parts.append(state["m0", u, a, h])
-                        col = slice((st * R + r) * P, (st * R + r + 1) * P)
-                        for n, part in enumerate(parts):
+        def turn_mix(u, h):
+            groups = [(0, 1)] if in_full(u, h) else [(0,), (1,)]
+            for g, ranks in enumerate(groups):
+                s = bank("s", [P, 2, T], 3)
+                for st in range(2):
+                    for a in range(2):
+                        terms = [(j, r) for j in range(2) for r in ranks]
+                        for n, (j, r) in enumerate(terms):
+                            col = slice(r * UNIT + st * P, r * UNIT + (st + 1) * P)
                             nc.tensor.matmul(
-                                s[:, h, a * P : (a + 1) * P], part[:, col], ident[:],
-                                start=(n == 0), stop=(n == len(parts) - 1), is_transpose=True,
+                                s[:, st, a * P : (a + 1) * P], state["m", u, a, j, h][:, col], ident[:],
+                                start=(n == 0), stop=(n == len(terms) - 1), is_transpose=True,
                             )
-                state["s", u, st, r] = s
+                state["s", u, h, g] = s
+            if in_full(u, h):
+                state["b", u, h] = state["s", u, h, 0]
 
-        def rank0(u, st):
-            s = state.pop(("s", u, st, 0))
-            b0 = buf("b0", 3, [P, H, T], F32)
-            for h in range(H):
-                nc.scalar.activation(b0[:, h, :], s[:, h, :], ACTF.Copy, scale=aq_neg[:, 2 * u + st, h, 0:1])
-            state["b0", u, st] = b0
+        def rank0(u, h):
+            if in_full(u, h):
+                return
+            s = state.pop(("s", u, h, 0))
+            b0 = buf("b0", 3, [P, 2, T], F32)
+            for st in range(2):
+                nc.scalar.activation(b0[:, st, :], s[:, st, :], ACTF.Copy, scale=aq_f[:, 2 * u + st, h, 0:1])
+            state["b0", u, h] = b0
 
-        def rank1(u, st):
-            s = state.pop(("s", u, st, 1))
-            b0 = state.pop(("b0", u, st))
-            b = buf("b", 3, [P, H, T], F32)
-            for h in range(H):
+        def rank1(u, h):
+            if in_full(u, h):
+                return
+            s = state.pop(("s", u, h, 1))
+            b0 = state.pop(("b0", u, h))
+            b = buf("b", 3, [P, 2, T], F32)
+            for st in range(2):
                 nc.vector.scalar_tensor_tensor(
-                    out=b[:, h, :], in0=s[:, h, :], scalar=aq_neg[:, 2 * u + st, h, 1:2], in1=b0[:, h, :],
+                    out=b[:, st, :], in0=s[:, st, :], scalar=aq_f[:, 2 * u + st, h, 1:2], in1=b0[:, st, :],
                     op0=ALU.mult, op1=ALU.add,
                 )
-            state["b", u, st] = b
+            state["b", u, h] = b
 
-        def row_max(u, st):
-            mn = buf("mn", 3, [P, H], F32, 32)
-            nc.vector.tensor_reduce(out=mn[:], in_=state["b", u, st][:], axis=AX.X, op=ALU.min)
-            state["mn", u, st] = mn
+        def row_max(u, h):
+            mn = buf("mn", 4, [P, 2], F32, 32)
+            nc.vector.tensor_reduce(out=mn[:], in_=state["b", u, h][:], axis=AX.X, op=ALU.min)
+            state["mn", u, h] = mn
 
-        def expo(u, st):
-            e = buf("e", 3, [P, H, T], F32)
-            sm = buf("sm", 3, [P, H], F32, 32)
-            b = state.pop(("b", u, st))
-            mn = state.pop(("mn", u, st))
-            for h in range(H):
+        def expo(u, h):
+            e = buf("e", 4, [P, 2, T], F32)
+            sm = buf("sm", 4, [P, 2], F32, 32)
+            b = state.pop(("b", u, h))
+            mn = state.pop(("mn", u, h))
+            for st in range(2):
                 nc.scalar.activation(
-                    e[:, h, :], b[:, h, :], ACTF.Exp, bias=mn[:, h : h + 1], scale=-1.0, accum_out=sm[:, h : h + 1]
+                    e[:, st, :], b[:, st, :], ACTF.Exp, bias=mn[:, st : st + 1], scale=-1.0,
+                    accum_out=sm[:, st : st + 1],
                 )
-            state["e", u, st] = (e, sm)
+            state["e", u, h] = (e, sm)
 
-        def recip(u, st):
-            rs = buf("rs", 3, [P, H], F32, 32)
-            nc.vector.reciprocal(rs[:], state["e", u, st][1][:])
-            state["rs", u, st] = rs
+        def recip(u, h):
+            rs = buf("rs", 4, [P, 2], F32, 32)
+            nc.vector.reciprocal(rs[:], state["e", u, h][1][:])
+            state["rs", u, h] = rs
 
-        def norm(u, st):
-            pn = buf("pn", 3, [P, H, T], F32)
-            e = state.pop(("e", u, st))[0]
-            rs = state.pop(("rs", u, st))
-            for h in range(H):
-                nc.vector.tensor_scalar(pn[:, h, :], e[:, h, :], rs[:, h : h + 1], None, op0=ALU.mult)
-            state["pn", u, st] = pn
+        def norm(u, h):
+            pn = buf("pn", 4, [P, 2, T], F32)
+            e = state.pop(("e", u, h))[0]
+            rs = state.pop(("rs", u, h))
+            for st in range(2):
+                nc.scalar.activation(pn[:, st, :], e[:, st, :], ACTF.Copy, scale=rs[:, st : st + 1])
+            state["pn", u, h] = pn
 
-        def turn_p(u, st):
-            pn = state.pop(("pn", u, st))
-            pt = bank("pt", [P, H, 2, P])
-            for h in range(H):
+        def turn_p(u, h):
+            pn = state.pop(("pn", u, h))
+            pt = bank("pt", [P, 2, 2, P], 1)
+            for st in range(2):
                 for a in range(2):
-                    nc.tensor.transpose(pt[:, h, a, :], pn[:, h, a * P : (a + 1) * P], ident[:])
-            state["pt", u, st] = pt
+                    nc.tensor.transpose(pt[:, a, st, :], pn[:, st, a * P : (a + 1) * P], ident[:])
+            state["pt", u, h] = pt
 
-        def weigh(u, st, h):
-            if ("ug", u, st) not in state:
-                state["ug", u, st] = buf("ug", 3, [P, H, P, 2, R], BF16)
+        def weigh(u, h):
+            ug = buf("ug", 3, [P, UNIT, 2, R], BF16)
             nc.vector.tensor_tensor(
-                out=state["ug", u, st][:, h],
-                in0=state["pt", u, st][:, h].rearrange("p a s -> p s a").unsqueeze(3).to_broadcast([P, P, 2, R]),
-                in1=av_f[:, h].unsqueeze(1).to_broadcast([P, P, 2, R]),
+                out=ug[:],
+                in0=state.pop(("pt", u, h))[:].rearrange("p a n s -> p (n s) a").unsqueeze(3).to_broadcast([P, UNIT, 2, R]),
+                in1=av_f[:, h].unsqueeze(1).to_broadcast([P, UNIT, 2, R]),
                 op=ALU.mult,
             )
+            state["ug", u, h] = ug
 
-        def quant_u(u, st):
-            ug = state.pop(("ug", u, st))
-            uc = buf("uc", 3, [P, H * P], U32)
-            us = buf("us", 3, [P, H * P], U8)
-            nc.vector.quantize_mx(
-                out=uc[:].bitcast(FP8X4), scales=us[:], in_=ug[:].rearrange("p h s a r -> p (h s a r)")
+        def quant_u(u, h):
+            ug = state.pop(("ug", u, h))
+            uc = buf("uc", 3, [P, UNIT], U32)
+            us = buf("us", 3, [P, UNIT], U8)
+            nc.vector.quantize_mx(out=uc[:].bitcast(FP8X4), scales=us[:], in_=ug[:].rearrange("p c a r -> p (c a r)"))
+            state["uq", u, h] = (uc, us)
+
+        def outs(u, h, st):
+            uc, us = state["uq", u, h]
+            o = bank("o", [P, K], 1)
+            col = slice(st * P, (st + 1) * P)
+            nc.tensor.matmul_mx(
+                out=o[:], lhsT=uc[:, col].bitcast(FP8X4), lhsT_scale=us[:, col],
+                rhs=vc[:].bitcast(FP8X4), rhs_scale=vs[:], start=True, stop=True,
             )
-            state["uq", u, st] = (uc, us)
+            state["o", u, h, st] = o
 
-        def outs(u, st):
-            uc, us = state.pop(("uq", u, st))
-            for h in range(H):
-                o = bank("o", [P, K], 2)
-                col = slice(h * P, (h + 1) * P)
-                nc.tensor.matmul_mx(
-                    out=o[:], lhsT=uc[:, col].bitcast(FP8X4), lhsT_scale=us[:, col],
-                    rhs=vc[:].bitcast(FP8X4), rhs_scale=vs[:], start=True, stop=True,
-                )
-                state["o", u, st, h] = o
+        out_view = out.rearrange("h (n p) k -> h p n k", p=P)
 
-        out_view = out.rearrange("h (p n) k -> n p h k", p=P)
-
-        def leave(u, st, h):
-            if ("ob", u, st) not in state:
-                state["ob", u, st] = buf("ob", 4, [P, H, K], F32)
-                state["left", u, st] = 0
-            ob = state["ob", u, st]
-            nc.scalar.copy(ob[:, h, :], state.pop(("o", u, st, h))[:])
-            state["left", u, st] += 1
-            if state["left", u, st] == H:
-                nc.sync.dma_start(out=out_view[2 * u + st], in_=ob[:])
+        def leave(u, h, st):
+            if ("ob", u, h) not in state:
+                state["ob", u, h] = buf("ob", 5, [P, 2, K], F32)
+                state["left", u, h] = 0
+            ob = state["ob", u, h]
+            nc.scalar.copy(ob[:, st, :], state.pop(("o", u, h, st))[:])
+            state["left", u, h] += 1
+            if state["left", u, h] == 2:
+                nc.sync.dma_start(out=out_view[h, :, 2 * u : 2 * u + 2, :], in_=ob[:])
 
         def step(fn, u, *rest):
             if 0 <= u < UNITS:
                 fn(u, *rest)
 
-        for i in range(-4, UNITS - (-1)):
-            if i == -4:
-                prep_k()
+        kg = prep_k()
+        for i in range(-2, UNITS - (-2)):
+            if i == -1:
+                prep_k_quant(kg)
+            if i == 1:
+                prep_v_quant()
+            step(row_max, i - 1, 1)
+            step(recip, i - 1, 0)
+            step(weigh, i - 2, 1)
+            step(dots, i, 1)
+            step(turn_x, i + 1, 1)
+            step(leave, i - 2, 0, 0)
+            step(mix, i, 1, 0, 0)
+            step(mix, i, 1, 1, 1)
+            step(outs, i - 2, 0, 1)
+            step(quant_u, i - 2, 1)
+            step(norm, i - 1, 0)
+            step(leave, i - 2, 0, 1)
+            step(mix, i, 1, 0, 1)
+            step(turn_p, i - 1, 0)
+            step(mix, i, 1, 1, 0)
+            step(outs, i - 2, 1, 0)
+            step(gather_x, i + 1, 1)
             if i == -1:
                 prep_v()
-            if i == 0:
-                prep_v_quant()
-            step(leave, i - 1, 0, 1)
-            step(weigh, i - 1, 1, 0)
-            step(recip, i, 0)
+            step(cast, i + 2)
+            step(turn_mix, i, 0)
+            step(turn_mix, i, 1)
+            step(quant_x, i + 1)
+            step(expo, i - 1, 1)
+            step(leave, i - 2, 1, 0)
+            step(turn_x, i + 2, 0)
+            step(recip, i - 1, 1)
+            step(weigh, i - 1, 0)
+            step(dots, i + 1, 0)
+            step(norm, i - 1, 1)
+            step(row_max, i, 0)
+            step(outs, i - 2, 1, 1)
+            step(quant_u, i - 1, 0)
             step(rank0, i, 1)
-            step(quant_u, i - 1, 1)
-            step(norm, i, 0)
+            step(mix, i + 1, 0, 0, 0)
+            step(mix, i + 1, 0, 1, 1)
+            step(leave, i - 2, 1, 1)
+            step(expo, i, 0)
+            step(turn_p, i - 1, 1)
+            step(outs, i - 1, 0, 0)
             step(rank1, i, 1)
-            step(mix1, i + 1, 0, 1)
-            step(outs, i - 1, 1)
-            step(gather_x, i + 2, 1)
-            step(dots, i + 1, 1)
-            step(cast, i + 3, 1)
-            step(leave, i - 1, 1, 1)
-            step(turn_p, i, 0)
-            step(turn_x, i + 3, 0)
-            step(row_max, i, 1)
-            step(weigh, i, 0, 1)
-            step(mix0, i + 1, 1, 0)
-            step(mix1, i + 1, 1, 1)
-            step(mix0, i + 1, 1, 1)
-            step(leave, i - 1, 1, 0)
-            step(expo, i, 1)
-            step(gather_x, i + 3, 0)
-            step(mix1, i + 1, 1, 0)
-            step(turn_f, i + 1, 0)
-            step(weigh, i, 0, 0)
-            step(quant_x, i + 2)
-            step(rank0, i + 1, 0)
-            step(quant_u, i, 0)
-            step(outs, i, 0)
-            step(leave, i, 0, 0)
-            step(dots, i + 2, 0)
-            step(cast, i + 4, 0)
-            step(mix0, i + 2, 0, 0)
-            step(recip, i, 1)
-            step(rank1, i + 1, 0)
-            step(norm, i, 1)
-            step(mix0, i + 2, 0, 1)
-            step(turn_p, i, 1)
-            step(row_max, i + 1, 0)
-            step(mix1, i + 2, 0, 0)
-            step(turn_f, i + 1, 1)
-            step(weigh, i, 1, 1)
-            step(expo, i + 1, 0)
-            step(turn_x, i + 3, 1)
+            step(mix, i + 1, 0, 0, 1)
+            step(mix, i + 1, 0, 1, 0)
+            step(gather_x, i + 2, 0)

@@ -23,6 +23,8 @@ ALU = mybir.AluOpType
 ACTF = mybir.ActivationFunctionType
 AX = mybir.AxisListType
 
+ON_GPSIMD = (0, 1)
+
 
 def tile_tensorproductfactordecode_t_kernel(tc, bq_bytes, bq_scale, aq, bk, ak, av, bv, out):
     nc = tc.nc
@@ -178,9 +180,9 @@ def tile_tensorproductfactordecode_t_kernel(tc, bq_bytes, bq_scale, aq, bk, ak, 
             return h == 0
 
         def mix(u, a, j, h):
-            m = buf(f"mix{h}", 10, [P, R * UNIT], F32)
+            m = buf(f"mix{h}", 8, [P, R * UNIT], F32)
             d = state["d", u, a, j]
-            if in_full(u, h):
+            if in_full(u, h) and not (j == 0 and a in ON_GPSIMD):
                 q0 = (u % AQ_UNITS) * UNIT
                 nc.vector.scalar_tensor_tensor(
                     out=m[:].rearrange("p (r c) -> p r c", r=R),
@@ -193,10 +195,21 @@ def tile_tensorproductfactordecode_t_kernel(tc, bq_bytes, bq_scale, aq, bk, ak, 
                 nc.scalar.activation(m[:], d[:], ACTF.Copy, scale=ak_neg[:, a, h, j : j + 1])
             state["m", u, a, j, h] = m
 
+        def mix_aq(u, a):
+            m = buf("mixq", 6, [P, R * UNIT], F32)
+            q0 = (u % AQ_UNITS) * UNIT
+            nc.gpsimd.tensor_tensor(
+                out=m[:].rearrange("p (r c) -> p r c", r=R),
+                in0=state["m", u, a, 0, 0][:].rearrange("p (r c) -> p r c", r=R),
+                in1=aq_cols[u // AQ_UNITS][:, q0 : q0 + UNIT, 0, :].rearrange("p c r -> p r c"),
+                op=ALU.mult,
+            )
+            state["m", u, a, 0, 0] = m
+
         def turn_mix(u, h):
             groups = [(0, 1)] if in_full(u, h) else [(0,), (1,)]
             for g, ranks in enumerate(groups):
-                s = bank("s", [P, 2, T], 3)
+                s = bank("s", [P, 2, T], 2)
                 for st in range(2):
                     for a in range(2):
                         terms = [(j, r) for j in range(2) for r in ranks]
@@ -259,7 +272,7 @@ def tile_tensorproductfactordecode_t_kernel(tc, bq_bytes, bq_scale, aq, bk, ak, 
             e = state.pop(("e", u, h))[0]
             rs = state.pop(("rs", u, h))
             for st in range(2):
-                nc.scalar.activation(pn[:, st, :], e[:, st, :], ACTF.Copy, scale=rs[:, st : st + 1])
+                nc.gpsimd.tensor_scalar(pn[:, st, :], e[:, st, :], rs[:, st : st + 1], 0.0, op0=ALU.mult, op1=ALU.add)
             state["pn", u, h] = pn
 
         def turn_p(u, h):
@@ -289,7 +302,7 @@ def tile_tensorproductfactordecode_t_kernel(tc, bq_bytes, bq_scale, aq, bk, ak, 
 
         def outs(u, h, st):
             uc, us = state["uq", u, h]
-            o = bank("o", [P, K], 1)
+            o = bank("o", [P, K], 2)
             col = slice(st * P, (st + 1) * P)
             nc.tensor.matmul_mx(
                 out=o[:], lhsT=uc[:, col].bitcast(FP8X4), lhsT_scale=us[:, col],
@@ -314,52 +327,54 @@ def tile_tensorproductfactordecode_t_kernel(tc, bq_bytes, bq_scale, aq, bk, ak, 
                 fn(u, *rest)
 
         kg = prep_k()
-        for i in range(-2, UNITS - (-2)):
-            if i == -1:
+        for i in range(-5, UNITS - (-3)):
+            if i == -2:
                 prep_k_quant(kg)
-            if i == 1:
+            if i == 2:
                 prep_v_quant()
-            step(row_max, i - 1, 1)
-            step(recip, i - 1, 0)
-            step(weigh, i - 2, 1)
-            step(dots, i, 1)
-            step(turn_x, i + 1, 1)
-            step(leave, i - 2, 0, 0)
-            step(mix, i, 1, 0, 0)
-            step(mix, i, 1, 1, 1)
-            step(outs, i - 2, 0, 1)
-            step(quant_u, i - 2, 1)
-            step(norm, i - 1, 0)
-            step(leave, i - 2, 0, 1)
-            step(mix, i, 1, 0, 1)
-            step(turn_p, i - 1, 0)
-            step(mix, i, 1, 1, 0)
-            step(outs, i - 2, 1, 0)
-            step(gather_x, i + 1, 1)
-            if i == -1:
-                prep_v()
-            step(cast, i + 2)
-            step(turn_mix, i, 0)
-            step(turn_mix, i, 1)
-            step(quant_x, i + 1)
-            step(expo, i - 1, 1)
-            step(leave, i - 2, 1, 0)
-            step(turn_x, i + 2, 0)
-            step(recip, i - 1, 1)
-            step(weigh, i - 1, 0)
-            step(dots, i + 1, 0)
-            step(norm, i - 1, 1)
-            step(row_max, i, 0)
-            step(outs, i - 2, 1, 1)
-            step(quant_u, i - 1, 0)
-            step(rank0, i, 1)
-            step(mix, i + 1, 0, 0, 0)
-            step(mix, i + 1, 0, 1, 1)
-            step(leave, i - 2, 1, 1)
-            step(expo, i, 0)
-            step(turn_p, i - 1, 1)
-            step(outs, i - 1, 0, 0)
-            step(rank1, i, 1)
-            step(mix, i + 1, 0, 0, 1)
             step(mix, i + 1, 0, 1, 0)
-            step(gather_x, i + 2, 0)
+            step(quant_u, i - 2, 0)
+            step(turn_p, i - 2, 1)
+            step(leave, i - 3, 0, 0)
+            step(leave, i - 3, 1, 1)
+            step(dots, i + 1, 1)
+            step(gather_x, i + 3, 1)
+            if i == -3:
+                prep_v()
+            step(cast, i + 5)
+            step(turn_x, i + 4, 0)
+            step(rank0, i, 1)
+            step(recip, i - 1, 0)
+            step(outs, i - 2, 0, 1)
+            step(mix, i + 1, 1, 1, 1)
+            step(mix_aq, i, 0)
+            step(turn_mix, i, 0)
+            step(mix, i + 1, 1, 0, 0)
+            step(mix, i + 1, 1, 0, 1)
+            step(expo, i - 1, 1)
+            step(weigh, i - 2, 1)
+            step(leave, i - 2, 0, 1)
+            step(norm, i - 1, 0)
+            step(turn_p, i - 1, 0)
+            step(rank1, i, 1)
+            step(outs, i - 3, 1, 0)
+            step(mix, i + 1, 1, 1, 0)
+            step(gather_x, i + 4, 0)
+            step(dots, i + 2, 0)
+            step(row_max, i, 0)
+            step(leave, i - 3, 1, 0)
+            step(quant_u, i - 2, 1)
+            step(mix_aq, i + 1, 1)
+            step(quant_x, i + 3)
+            step(turn_x, i + 4, 1)
+            step(outs, i - 2, 0, 0)
+            step(recip, i - 1, 1)
+            step(expo, i, 0)
+            step(mix, i + 2, 0, 1, 1)
+            step(outs, i - 2, 1, 1)
+            step(weigh, i - 1, 0)
+            step(mix, i + 2, 0, 0, 0)
+            step(norm, i - 1, 1)
+            step(mix, i + 2, 0, 0, 1)
+            step(turn_mix, i + 1, 1)
+            step(row_max, i, 1)

@@ -6,9 +6,13 @@ from concourse.masks import make_identity
 
 S, T, H, R, K = 4096, 256, 2, 2, 512
 P = 128
-TILES = S // P
-UNITS = TILES // 2
-UNIT = 2 * P
+PACK = 4
+HALVES = 2
+TILES = 2
+UNIT = TILES * P
+UNITS = S // UNIT
+COLS = R * UNIT
+ROW = R * K
 AQ_UNITS = 2
 
 FLOPS = 2 * 2 * (S * R) * (T * R) * K
@@ -20,10 +24,12 @@ U8 = mybir.dt.uint8
 FP8 = mybir.dt.float8_e4m3fn
 FP8X4 = mybir.dt.float8_e4m3fn_x4
 ALU = mybir.AluOpType
-ACTF = mybir.ActivationFunctionType
-AX = mybir.AxisListType
+ACT = mybir.ActivationFunctionType
+AXIS = mybir.AxisListType
 
-ON_GPSIMD = (0, 1)
+
+def shared_on_gpsimd(u):
+    return 3 <= u < UNITS - 4
 
 
 def tile_tensorproductfactordecode_t_kernel(tc, bq_bytes, bq_scale, aq, bk, ak, av, bv, out):
@@ -38,22 +44,29 @@ def tile_tensorproductfactordecode_t_kernel(tc, bq_bytes, bq_scale, aq, bk, ak, 
 
         ctx.enter_context(tc.manual_schedule())
 
-        x_view = bq_bytes.rearrange("(n p) r k -> p n (r k)", p=P)
-        x_tiles = [keep.tile([P, 2 * R * K], U8, name=f"xb{u}", align_bytes=64) for u in range(UNITS)]
-        scale_row = keep.tile([P, 2 * R * K], F32, name="scale_row")
-        aq_cols = [keep.tile([P, AQ_UNITS * UNIT, H, R], BF16, name=f"aqc{c}") for c in range(UNITS // AQ_UNITS)]
-        aq_raw = keep.tile([P, TILES, H * R], BF16, name="aq_raw")
-        ak_raw = keep.tile([P, 2 * H * R], BF16, name="ak_raw")
-        av_raw = keep.tile([P, 2 * H * R], BF16, name="av_raw")
-        bk_raw = keep.tile([P, 4, K], BF16, name="bk_raw", align_bytes=64)
-        bv_raw = keep.tile([P, 4, K], BF16, name="bv_raw", align_bytes=64)
+        def buf(tag, bufs, shape, dtype, align=64):
+            return work.tile(shape, dtype, name=tag, tag=tag, bufs=bufs, align_bytes=align)
 
-        def load_x(u):
-            nc.sync.dma_start(
-                out=x_tiles[u][:].rearrange("p (n c) -> p n c", n=2), in_=x_view[:, 2 * u : 2 * u + 2, :]
-            )
+        def bank(tag, bufs, shape):
+            return psum.tile(shape, F32, name=tag, tag=tag, bufs=bufs)
 
+        bq_tiles = [keep.tile([P, TILES * ROW], U8, name=f"bq{u}", align_bytes=64) for u in range(UNITS)]
+        scales = keep.tile([P, TILES * ROW], F32, name="scales")
+        aq_cols = [keep.tile([P, AQ_UNITS * UNIT, H, R], BF16, name=f"aq_cols{c}") for c in range(UNITS // AQ_UNITS)]
+        aq_raw = keep.tile([P, S // P, H * R], BF16, name="aq_raw")
+        ak_raw = keep.tile([P, HALVES * H * R], BF16, name="ak_raw")
+        av_raw = keep.tile([P, HALVES * H * R], BF16, name="av_raw")
+        bk_raw = keep.tile([P, PACK, K], BF16, name="bk_raw", align_bytes=64)
+        bv_raw = keep.tile([P, PACK, K], BF16, name="bv_raw", align_bytes=64)
+
+        bq_view = bq_bytes.rearrange("(n p) r k -> p n (r k)", p=P)
         aq_flat = aq.rearrange("s h r -> (s h r)")
+
+        def load_bq(u):
+            nc.sync.dma_start(
+                out=bq_tiles[u][:].rearrange("p (n c) -> p n c", n=TILES),
+                in_=bq_view[:, TILES * u : TILES * (u + 1), :],
+            )
 
         def load_aq(c):
             n = AQ_UNITS * UNIT * H * R
@@ -62,319 +75,349 @@ def tile_tensorproductfactordecode_t_kernel(tc, bq_bytes, bq_scale, aq, bk, ak, 
                 in_=aq_flat[c * n : (c + 1) * n].partition_broadcast(P),
             )
 
-        load_x(0)
-        nc.scalar.dma_start(out=scale_row[:, 0:K], in_=bq_scale.rearrange("a b k -> (a b k)").partition_broadcast(P))
-        nc.sync.dma_start(out=bk_raw[:].rearrange("p x k -> p (x k)"), in_=bk.rearrange("(p tt) j k -> p (tt j k)", p=P))
-        nc.scalar.dma_start(out=ak_raw[:], in_=ak.rearrange("(p tt) h j -> p (tt h j)", p=P))
-        nc.scalar.dma_start(out=av_raw[:], in_=av.rearrange("(p tt) h r -> p (tt h r)", p=P))
+        load_bq(0)
+        nc.scalar.dma_start(out=scales[:, 0:K], in_=bq_scale.rearrange("a b k -> (a b k)").partition_broadcast(P))
+        nc.sync.dma_start(out=bk_raw[:].rearrange("p x k -> p (x k)"), in_=bk.rearrange("(p a) j k -> p (a j k)", p=P))
+        nc.scalar.dma_start(out=ak_raw[:], in_=ak.rearrange("(p a) h j -> p (a h j)", p=P))
+        nc.scalar.dma_start(out=av_raw[:], in_=av.rearrange("(p a) h r -> p (a h r)", p=P))
         load_aq(0)
-        load_x(1)
+        load_bq(1)
         nc.sync.dma_start(out=aq_raw[:], in_=aq.rearrange("(n p) h r -> p n (h r)", p=P))
-        nc.sync.dma_start(out=bv_raw[:].rearrange("p x k -> p (x k)"), in_=bv.rearrange("(p tt) r k -> p (tt r k)", p=P))
-        for u in range(2, UNITS):
-            load_x(u)
-            if u % 2 == 0:
-                load_aq(u // 2)
+        nc.sync.dma_start(out=bv_raw[:].rearrange("p x k -> p (x k)"), in_=bv.rearrange("(p a) r k -> p (a r k)", p=P))
+        for u in range(AQ_UNITS, UNITS):
+            load_bq(u)
+            if u % AQ_UNITS == 0:
+                load_aq(u // AQ_UNITS)
 
         warm = keep.tile([P, 1], F32, name="warm")
         nc.vector.memset(warm[:], 0.0)
         warm_out = keep.tile([P, 1], F32, name="warm_out")
-        nc.scalar.activation(warm_out[:], warm[:], ACTF.Exp)
-        nc.vector.tensor_copy(scale_row[:, K : 2 * K], scale_row[:, 0:K])
-        nc.vector.tensor_copy(scale_row[:, 2 * K : 4 * K], scale_row[:, 0 : 2 * K])
-        ak_neg = keep.tile([P, 2, H, R], F32, name="ak_neg")
+        nc.scalar.activation(warm_out[:], warm[:], ACT.Exp)
+
+        nc.vector.tensor_copy(scales[:, K : 2 * K], scales[:, 0:K])
+        nc.vector.tensor_copy(scales[:, 2 * K : 4 * K], scales[:, 0 : 2 * K])
+
+        ak_neg = keep.tile([P, HALVES, H, R], F32, name="ak_neg")
         nc.gpsimd.tensor_scalar(
             ak_neg[:].rearrange("p a h j -> p (a h j)"), ak_raw[:], -1.0 / math.sqrt(K), 0.0, op0=ALU.mult, op1=ALU.add
         )
-        av_f = keep.tile([P, H, 2, R], F32, name="av_f")
-        nc.gpsimd.tensor_copy(av_f[:], av_raw[:].rearrange("p (a h r) -> p h a r", a=2, h=H))
-        aq_f = keep.tile([P, TILES, H, R], F32, name="aq_f")
-        nc.gpsimd.tensor_copy(out=aq_f[:].rearrange("p n h r -> p (n h r)"), in_=aq_raw[:].rearrange("p n c -> p (n c)"))
+        av_f = keep.tile([P, H, HALVES, R], F32, name="av_f")
+        nc.gpsimd.tensor_copy(av_f[:], av_raw[:].rearrange("p (a h r) -> p h a r", a=HALVES, h=H))
+        aq_f = keep.tile([P, S // P, H, R], F32, name="aq_f")
+        nc.gpsimd.tensor_copy(
+            out=aq_f[:].rearrange("p n h r -> p (n h r)"), in_=aq_raw[:].rearrange("p n c -> p (n c)")
+        )
 
-        kc = keep.tile([P, 4 * P], U32, name="kc", align_bytes=64)
-        ks = keep.tile([P, 4 * P], U8, name="ks", align_bytes=64)
-        vc = keep.tile([P, K], U32, name="vc", align_bytes=64)
-        vs = keep.tile([P, K], U8, name="vs", align_bytes=64)
+        bk_codes = keep.tile([P, PACK * P], U32, name="bk_codes", align_bytes=64)
+        bk_bytes = keep.tile([P, PACK * P], U8, name="bk_bytes", align_bytes=64)
+        bv_codes = keep.tile([P, K], U32, name="bv_codes", align_bytes=64)
+        bv_bytes = keep.tile([P, K], U8, name="bv_bytes", align_bytes=64)
+        bk_packed = keep.tile([P, PACK * P * PACK], BF16, name="bk_packed", align_bytes=64)
+        bv_packed = keep.tile([P, K, PACK], BF16, name="bv_packed", align_bytes=64)
 
-        def bank(tag, shape, bufs):
-            return psum.tile(shape, F32, name=tag, tag=tag, bufs=bufs)
+        def transpose_words(dst, words, base):
+            for w in range(2):
+                nc.tensor.transpose(dst(w), words[:, base + w : base + K // 2 : 2], ident[:])
 
-        def buf(tag, bufs, shape, dtype, align=64):
-            return work.tile(shape, dtype, name=tag, tag=tag, bufs=bufs, align_bytes=align)
-
-        state = {}
-
-        def words_of(tile_ap):
-            return tile_ap.bitcast(F32).rearrange("p (c u) -> p c u", u=2)
-
-        def prep_k():
-            kg = keep.tile([P, 4 * P, 4], BF16, name="kg", align_bytes=64)
-            kgw = words_of(kg[:].rearrange("p c t -> p (c t)"))
+        def turn_bk():
             words = bk_raw[:].rearrange("p x k -> p (x k)").bitcast(F32)
-            for half in range(2):
-                kt = bank("xt", [P, 2, 2 * P], 1)
-                for x2 in range(2):
-                    for u in range(2):
-                        base = (2 * half + x2) * (K // 2)
-                        nc.tensor.transpose(
-                            kt[:, u, x2 * P : (x2 + 1) * P], words[:, base + u : base + K // 2 : 2], ident[:]
-                        )
+            packed = bk_packed[:].bitcast(F32).rearrange("p (c w) -> p c w", w=2)
+            for pair in range(2):
+                turned = bank("o", 2, [P, 2, 2 * P])
+                for x in range(2):
+                    cols = slice(x * P, (x + 1) * P)
+                    transpose_words(lambda w: turned[:, w, cols], words, (2 * pair + x) * (K // 2))
                 nc.scalar.copy(
-                    out=kgw[:, half * 2 * P : (half + 1) * 2 * P, :], in_=kt[:].rearrange("p u c -> p c u")
+                    out=packed[:, pair * 2 * P : (pair + 1) * 2 * P, :], in_=turned[:].rearrange("p w c -> p c w")
                 )
-            return kg
 
-        def prep_k_quant(kg):
-            nc.vector.quantize_mx(out=kc[:].bitcast(FP8X4), scales=ks[:], in_=kg[:].rearrange("p c t -> p (c t)"))
+        def quantize_bk():
+            nc.vector.quantize_mx(out=bk_codes[:].bitcast(FP8X4), scales=bk_bytes[:], in_=bk_packed[:])
 
-        vg = keep.tile([P, K, 4], BF16, name="vg", align_bytes=64)
+        def pack_bv(quarter):
+            n = slice(quarter * P, (quarter + 1) * P)
+            nc.scalar.copy(out=bv_packed[:, n, :], in_=bv_raw[:, :, n].rearrange("p x n -> p n x"))
 
-        def prep_v():
-            nc.scalar.copy(out=vg[:], in_=bv_raw[:].rearrange("p j n -> p n j"))
+        def quantize_bv():
+            nc.vector.quantize_mx(
+                out=bv_codes[:].bitcast(FP8X4), scales=bv_bytes[:], in_=bv_packed[:].rearrange("p n x -> p (n x)")
+            )
 
-        def prep_v_quant():
-            nc.vector.quantize_mx(out=vc[:].bitcast(FP8X4), scales=vs[:], in_=vg[:].rearrange("p n t -> p (n t)"))
+        live = {}
 
-        def cast(u):
-            xw = buf("xw", 4, [P, 2 * R * K], BF16)
-            nc.vector.tensor_tensor(out=xw[:], in0=x_tiles[u][:].bitcast(FP8), in1=scale_row[:], op=ALU.mult)
-            state["xw", u] = xw
+        def scale_bq(u):
+            bq = buf("bq", 4, [P, TILES * ROW], BF16)
+            nc.vector.tensor_tensor(out=bq[:], in0=bq_tiles[u][:].bitcast(FP8), in1=scales[:], op=ALU.mult)
+            live["bq", u] = bq
 
-        def turn_x(u, st):
-            words = state["xw", u][:].bitcast(F32)
-            xt = bank("xt", [P, 2, R * P], 1)
+        def turn_bq(u, tile):
+            words = live["bq", u][:].bitcast(F32)
+            turned = bank("bq_turned", 1, [P, 2, R * P])
             for r in range(R):
-                for w in range(2):
-                    base = (st * R + r) * (K // 2)
-                    nc.tensor.transpose(
-                        xt[:, w, r * P : (r + 1) * P], words[:, base + w : base + K // 2 : 2], ident[:]
-                    )
-            state["xt", u, st] = xt
+                cols = slice(r * P, (r + 1) * P)
+                transpose_words(lambda w: turned[:, w, cols], words, (tile * R + r) * (K // 2))
+            live["turned", u, tile] = turned
 
-        def gather_x(u, st):
-            if ("xg", u) not in state:
-                state["xg", u] = buf("xg", 2, [P, R * 2 * P * 4], BF16)
-            xt = state.pop(("xt", u, st))
-            xgw = state["xg", u][:].bitcast(F32).rearrange("p (r n s w) -> p r n s w", r=R, n=2, w=2)
-            nc.scalar.copy(xgw[:, :, st, :, :], xt[:].rearrange("p w (r s) -> p r s w", r=R))
+        def pack_bq(u, tile):
+            if ("packed", u) not in live:
+                live["packed", u] = buf("packed", 2, [P, COLS * PACK], BF16)
+            packed = live["packed", u][:].bitcast(F32).rearrange("p (r n s w) -> p r n s w", r=R, n=TILES, w=2)
+            nc.scalar.copy(
+                packed[:, :, tile, :, :], live.pop(("turned", u, tile))[:].rearrange("p w (r s) -> p r s w", r=R)
+            )
 
-        def quant_x(u):
-            xg = state.pop(("xg", u))
-            xc = buf("xc", 2, [P, 4 * P], U32)
-            xs = buf("xs", 2, [P, 4 * P], U8)
-            nc.vector.quantize_mx(out=xc[:].bitcast(FP8X4), scales=xs[:], in_=xg[:])
-            state["xq", u] = (xc, xs)
+        def quantize_bq(u):
+            codes = buf("codes", 2, [P, COLS], U32)
+            scale_bytes = buf("scale_bytes", 2, [P, COLS], U8)
+            nc.vector.quantize_mx(
+                out=codes[:].bitcast(FP8X4), scales=scale_bytes[:], in_=live.pop(("packed", u))[:]
+            )
+            live["bq_mx", u] = (codes, scale_bytes)
 
-        def dots(u, a):
-            xc, xs = state["xq", u]
-            for j in range(2):
-                d = bank(f"d{j}", [P, 4 * P], 1)
-                col = slice((2 * a + j) * P, (2 * a + j + 1) * P)
+        def dot(u, a):
+            codes, scale_bytes = live["bq_mx", u]
+            for j in range(R):
+                dots = bank(f"dot{j}", 1, [P, COLS])
+                cols = slice((2 * a + j) * P, (2 * a + j + 1) * P)
                 nc.tensor.matmul_mx(
-                    out=d[:], lhsT=kc[:, col].bitcast(FP8X4), lhsT_scale=ks[:, col],
-                    rhs=xc[:].bitcast(FP8X4), rhs_scale=xs[:], start=True, stop=True,
+                    out=dots[:],
+                    lhsT=bk_codes[:, cols].bitcast(FP8X4),
+                    lhsT_scale=bk_bytes[:, cols],
+                    rhs=codes[:].bitcast(FP8X4),
+                    rhs_scale=scale_bytes[:],
+                    start=True,
+                    stop=True,
                 )
-                state["d", u, a, j] = d
+                live["dot", u, a, j] = dots
 
-        def in_full(u, h):
-            return h == 0
+        def aq_of_head_0(u):
+            first = (u % AQ_UNITS) * UNIT
+            return aq_cols[u // AQ_UNITS][:, first : first + UNIT, 0, :].rearrange("p c r -> p r c")
+
+        def by_rank(tile_ap):
+            return tile_ap.rearrange("p (r c) -> p r c", r=R)
 
         def mix(u, a, j, h):
-            m = buf(f"mix{h}", 8, [P, R * UNIT], F32)
-            d = state["d", u, a, j]
-            if in_full(u, h) and not (j == 0 and a in ON_GPSIMD):
-                q0 = (u % AQ_UNITS) * UNIT
+            term = buf(f"term{h}", 8, [P, COLS], F32)
+            dots = live["dot", u, a, j]
+            factor = ak_neg[:, a, h, j : j + 1]
+            if h == 0 and not (j == 0 and shared_on_gpsimd(u)):
                 nc.vector.scalar_tensor_tensor(
-                    out=m[:].rearrange("p (r c) -> p r c", r=R),
-                    in0=d[:].rearrange("p (r c) -> p r c", r=R),
-                    scalar=ak_neg[:, a, h, j : j + 1],
-                    in1=aq_cols[u // AQ_UNITS][:, q0 : q0 + UNIT, h, :].rearrange("p c r -> p r c"),
-                    op0=ALU.mult, op1=ALU.mult,
+                    out=by_rank(term[:]),
+                    in0=by_rank(dots[:]),
+                    scalar=factor,
+                    in1=aq_of_head_0(u),
+                    op0=ALU.mult,
+                    op1=ALU.mult,
                 )
             else:
-                nc.scalar.activation(m[:], d[:], ACTF.Copy, scale=ak_neg[:, a, h, j : j + 1])
-            state["m", u, a, j, h] = m
+                nc.scalar.activation(term[:], dots[:], ACT.Copy, scale=factor)
+            live["term", u, a, j, h] = term
 
         def mix_aq(u, a):
-            m = buf("mixq", 6, [P, R * UNIT], F32)
-            q0 = (u % AQ_UNITS) * UNIT
+            if not shared_on_gpsimd(u):
+                return
+            term = buf("term_aq", 6, [P, COLS], F32)
             nc.gpsimd.tensor_tensor(
-                out=m[:].rearrange("p (r c) -> p r c", r=R),
-                in0=state["m", u, a, 0, 0][:].rearrange("p (r c) -> p r c", r=R),
-                in1=aq_cols[u // AQ_UNITS][:, q0 : q0 + UNIT, 0, :].rearrange("p c r -> p r c"),
-                op=ALU.mult,
+                out=by_rank(term[:]), in0=by_rank(live["term", u, a, 0, 0][:]), in1=aq_of_head_0(u), op=ALU.mult
             )
-            state["m", u, a, 0, 0] = m
+            live["term", u, a, 0, 0] = term
 
-        def turn_mix(u, h):
-            groups = [(0, 1)] if in_full(u, h) else [(0,), (1,)]
+        def turn_terms(u, h):
+            groups = [range(R)] if h == 0 else [(r,) for r in range(R)]
             for g, ranks in enumerate(groups):
-                s = bank("s", [P, 2, T], 2)
-                for st in range(2):
-                    for a in range(2):
-                        terms = [(j, r) for j in range(2) for r in ranks]
-                        for n, (j, r) in enumerate(terms):
-                            col = slice(r * UNIT + st * P, r * UNIT + (st + 1) * P)
+                scores = bank("scores", 2, [P, TILES, T])
+                for tile in range(TILES):
+                    for a in range(HALVES):
+                        summed = [(j, r) for j in range(R) for r in ranks]
+                        for n, (j, r) in enumerate(summed):
+                            first = r * UNIT + tile * P
                             nc.tensor.matmul(
-                                s[:, st, a * P : (a + 1) * P], state["m", u, a, j, h][:, col], ident[:],
-                                start=(n == 0), stop=(n == len(terms) - 1), is_transpose=True,
+                                scores[:, tile, a * P : (a + 1) * P],
+                                live["term", u, a, j, h][:, first : first + P],
+                                ident[:],
+                                start=(n == 0),
+                                stop=(n == len(summed) - 1),
+                                is_transpose=True,
                             )
-                state["s", u, h, g] = s
-            if in_full(u, h):
-                state["b", u, h] = state["s", u, h, 0]
+                live["sum", u, h, g] = scores
+            if h == 0:
+                live["score", u, 0] = live["sum", u, 0, 0]
 
-        def rank0(u, h):
-            if in_full(u, h):
-                return
-            s = state.pop(("s", u, h, 0))
-            b0 = buf("b0", 3, [P, 2, T], F32)
-            for st in range(2):
-                nc.scalar.activation(b0[:, st, :], s[:, st, :], ACTF.Copy, scale=aq_f[:, 2 * u + st, h, 0:1])
-            state["b0", u, h] = b0
-
-        def rank1(u, h):
-            if in_full(u, h):
-                return
-            s = state.pop(("s", u, h, 1))
-            b0 = state.pop(("b0", u, h))
-            b = buf("b", 3, [P, 2, T], F32)
-            for st in range(2):
-                nc.vector.scalar_tensor_tensor(
-                    out=b[:, st, :], in0=s[:, st, :], scalar=aq_f[:, 2 * u + st, h, 1:2], in1=b0[:, st, :],
-                    op0=ALU.mult, op1=ALU.add,
+        def rank_0(u):
+            part = buf("part", 3, [P, TILES, T], F32)
+            summed = live.pop(("sum", u, 1, 0))
+            for tile in range(TILES):
+                nc.scalar.activation(
+                    part[:, tile, :], summed[:, tile, :], ACT.Copy, scale=aq_f[:, TILES * u + tile, 1, 0:1]
                 )
-            state["b", u, h] = b
+            live["part", u] = part
+
+        def rank_1(u):
+            score = buf("score", 3, [P, TILES, T], F32)
+            summed = live.pop(("sum", u, 1, 1))
+            part = live.pop(("part", u))
+            for tile in range(TILES):
+                nc.vector.scalar_tensor_tensor(
+                    out=score[:, tile, :],
+                    in0=summed[:, tile, :],
+                    scalar=aq_f[:, TILES * u + tile, 1, 1:2],
+                    in1=part[:, tile, :],
+                    op0=ALU.mult,
+                    op1=ALU.add,
+                )
+            live["score", u, 1] = score
 
         def row_max(u, h):
-            mn = buf("mn", 4, [P, 2], F32, 32)
-            nc.vector.tensor_reduce(out=mn[:], in_=state["b", u, h][:], axis=AX.X, op=ALU.min)
-            state["mn", u, h] = mn
+            lowest = buf("lowest", 4, [P, TILES], F32, 32)
+            nc.vector.tensor_reduce(out=lowest[:], in_=live["score", u, h][:], axis=AXIS.X, op=ALU.min)
+            live["lowest", u, h] = lowest
 
         def expo(u, h):
-            e = buf("e", 4, [P, 2, T], F32)
-            sm = buf("sm", 4, [P, 2], F32, 32)
-            b = state.pop(("b", u, h))
-            mn = state.pop(("mn", u, h))
-            for st in range(2):
+            e = buf("e", 4, [P, TILES, T], F32)
+            total = buf("total", 4, [P, TILES], F32, 32)
+            score = live.pop(("score", u, h))
+            lowest = live.pop(("lowest", u, h))
+            for tile in range(TILES):
                 nc.scalar.activation(
-                    e[:, st, :], b[:, st, :], ACTF.Exp, bias=mn[:, st : st + 1], scale=-1.0,
-                    accum_out=sm[:, st : st + 1],
+                    e[:, tile, :],
+                    score[:, tile, :],
+                    ACT.Exp,
+                    bias=lowest[:, tile : tile + 1],
+                    scale=-1.0,
+                    accum_out=total[:, tile : tile + 1],
                 )
-            state["e", u, h] = (e, sm)
+            live["e", u, h] = (e, total)
 
         def recip(u, h):
-            rs = buf("rs", 4, [P, 2], F32, 32)
-            nc.vector.reciprocal(rs[:], state["e", u, h][1][:])
-            state["rs", u, h] = rs
+            inverse = buf("inverse", 4, [P, TILES], F32, 32)
+            nc.vector.reciprocal(inverse[:], live["e", u, h][1][:])
+            live["inverse", u, h] = inverse
 
         def norm(u, h):
-            pn = buf("pn", 4, [P, 2, T], F32)
-            e = state.pop(("e", u, h))[0]
-            rs = state.pop(("rs", u, h))
-            for st in range(2):
-                nc.gpsimd.tensor_scalar(pn[:, st, :], e[:, st, :], rs[:, st : st + 1], 0.0, op0=ALU.mult, op1=ALU.add)
-            state["pn", u, h] = pn
+            prob = buf("prob", 4, [P, TILES, T], F32)
+            e = live.pop(("e", u, h))[0]
+            inverse = live.pop(("inverse", u, h))
+            for tile in range(TILES):
+                by = inverse[:, tile : tile + 1]
+                if u < UNITS - 1:
+                    nc.gpsimd.tensor_scalar(prob[:, tile, :], e[:, tile, :], by, 0.0, op0=ALU.mult, op1=ALU.add)
+                else:
+                    nc.vector.tensor_scalar(prob[:, tile, :], e[:, tile, :], by, None, op0=ALU.mult)
+            live["prob", u, h] = prob
 
         def turn_p(u, h):
-            pn = state.pop(("pn", u, h))
-            pt = bank("pt", [P, 2, 2, P], 1)
-            for st in range(2):
-                for a in range(2):
-                    nc.tensor.transpose(pt[:, a, st, :], pn[:, st, a * P : (a + 1) * P], ident[:])
-            state["pt", u, h] = pt
+            prob = live.pop(("prob", u, h))
+            turned = bank("p_turned", 1, [P, HALVES, TILES, P])
+            for tile in range(TILES):
+                for a in range(HALVES):
+                    nc.tensor.transpose(turned[:, a, tile, :], prob[:, tile, a * P : (a + 1) * P], ident[:])
+            live["p_turned", u, h] = turned
 
         def weigh(u, h):
-            ug = buf("ug", 3, [P, UNIT, 2, R], BF16)
+            weighted = buf("weighted", 3, [P, UNIT, HALVES, R], BF16)
+            turned = live.pop(("p_turned", u, h))
+            shape = [P, UNIT, HALVES, R]
             nc.vector.tensor_tensor(
-                out=ug[:],
-                in0=state.pop(("pt", u, h))[:].rearrange("p a n s -> p (n s) a").unsqueeze(3).to_broadcast([P, UNIT, 2, R]),
-                in1=av_f[:, h].unsqueeze(1).to_broadcast([P, UNIT, 2, R]),
+                out=weighted[:],
+                in0=turned[:].rearrange("p a n s -> p (n s) a").unsqueeze(3).to_broadcast(shape),
+                in1=av_f[:, h].unsqueeze(1).to_broadcast(shape),
                 op=ALU.mult,
             )
-            state["ug", u, h] = ug
+            live["weighted", u, h] = weighted
 
-        def quant_u(u, h):
-            ug = state.pop(("ug", u, h))
-            uc = buf("uc", 3, [P, UNIT], U32)
-            us = buf("us", 3, [P, UNIT], U8)
-            nc.vector.quantize_mx(out=uc[:].bitcast(FP8X4), scales=us[:], in_=ug[:].rearrange("p c a r -> p (c a r)"))
-            state["uq", u, h] = (uc, us)
-
-        def outs(u, h, st):
-            uc, us = state["uq", u, h]
-            o = bank("o", [P, K], 2)
-            col = slice(st * P, (st + 1) * P)
-            nc.tensor.matmul_mx(
-                out=o[:], lhsT=uc[:, col].bitcast(FP8X4), lhsT_scale=us[:, col],
-                rhs=vc[:].bitcast(FP8X4), rhs_scale=vs[:], start=True, stop=True,
+        def quantize_u(u, h):
+            codes = buf("u_codes", 3, [P, UNIT], U32)
+            scale_bytes = buf("u_bytes", 3, [P, UNIT], U8)
+            nc.vector.quantize_mx(
+                out=codes[:].bitcast(FP8X4),
+                scales=scale_bytes[:],
+                in_=live.pop(("weighted", u, h))[:].rearrange("p c a r -> p (c a r)"),
             )
-            state["o", u, h, st] = o
+            live["u_mx", u, h] = (codes, scale_bytes)
+
+        def multiply_bv(u, h, tile):
+            codes, scale_bytes = live["u_mx", u, h]
+            result = bank("o", 2, [P, K])
+            cols = slice(tile * P, (tile + 1) * P)
+            nc.tensor.matmul_mx(
+                out=result[:],
+                lhsT=codes[:, cols].bitcast(FP8X4),
+                lhsT_scale=scale_bytes[:, cols],
+                rhs=bv_codes[:].bitcast(FP8X4),
+                rhs_scale=bv_bytes[:],
+                start=True,
+                stop=True,
+            )
+            live["result", u, h, tile] = result
 
         out_view = out.rearrange("h (n p) k -> h p n k", p=P)
 
-        def leave(u, h, st):
-            if ("ob", u, h) not in state:
-                state["ob", u, h] = buf("ob", 5, [P, 2, K], F32)
-                state["left", u, h] = 0
-            ob = state["ob", u, h]
-            nc.scalar.copy(ob[:, st, :], state.pop(("o", u, h, st))[:])
-            state["left", u, h] += 1
-            if state["left", u, h] == 2:
-                nc.sync.dma_start(out=out_view[h, :, 2 * u : 2 * u + 2, :], in_=ob[:])
+        def leave(u, h, tile):
+            if ("stage", u, h) not in live:
+                live["stage", u, h] = buf("stage", 5, [P, TILES, K], F32)
+                live["left", u, h] = 0
+            stage = live["stage", u, h]
+            nc.scalar.copy(stage[:, tile, :], live.pop(("result", u, h, tile))[:])
+            live["left", u, h] += 1
+            if u == UNITS - 1:
+                nc.sync.dma_start(out=out_view[h, :, TILES * u + tile, :], in_=stage[:, tile, :])
+            elif live["left", u, h] == TILES:
+                nc.sync.dma_start(out=out_view[h, :, TILES * u : TILES * (u + 1), :], in_=stage[:])
 
-        def step(fn, u, *rest):
+        def step(do, u, *rest):
             if 0 <= u < UNITS:
-                fn(u, *rest)
+                do(u, *rest)
 
-        kg = prep_k()
-        for i in range(-5, UNITS - (-3)):
+        turn_bk()
+        for i in range(-5, UNITS + 3):
             if i == -2:
-                prep_k_quant(kg)
+                quantize_bk()
             if i == 2:
-                prep_v_quant()
-            step(mix, i + 1, 0, 1, 0)
-            step(quant_u, i - 2, 0)
-            step(turn_p, i - 2, 1)
+                quantize_bv()
+            if -3 <= i < 1:
+                pack_bv(i + 3)
             step(leave, i - 3, 0, 0)
+            step(multiply_bv, i - 3, 1, 1)
+            step(row_max, i - 1, 1)
+            step(turn_terms, i, 1)
+            step(mix, i + 1, 0, 1, 0)
+            step(pack_bq, i + 3, 1)
             step(leave, i - 3, 1, 1)
-            step(dots, i + 1, 1)
-            step(gather_x, i + 3, 1)
-            if i == -3:
-                prep_v()
-            step(cast, i + 5)
-            step(turn_x, i + 4, 0)
-            step(rank0, i, 1)
+            step(turn_p, i - 2, 1)
+            step(dot, i + 1, 1)
+            step(quantize_u, i - 2, 0)
             step(recip, i - 1, 0)
-            step(outs, i - 2, 0, 1)
-            step(mix, i + 1, 1, 1, 1)
-            step(mix_aq, i, 0)
-            step(turn_mix, i, 0)
+            step(multiply_bv, i - 2, 0, 1)
+            step(scale_bq, i + 5)
             step(mix, i + 1, 1, 0, 0)
-            step(mix, i + 1, 1, 0, 1)
-            step(expo, i - 1, 1)
+            step(rank_0, i)
             step(weigh, i - 2, 1)
-            step(leave, i - 2, 0, 1)
+            step(mix, i + 1, 1, 1, 1)
+            step(multiply_bv, i - 3, 1, 0)
+            step(mix_aq, i, 0)
+            step(mix, i + 1, 1, 0, 1)
             step(norm, i - 1, 0)
-            step(turn_p, i - 1, 0)
-            step(rank1, i, 1)
-            step(outs, i - 3, 1, 0)
             step(mix, i + 1, 1, 1, 0)
-            step(gather_x, i + 4, 0)
-            step(dots, i + 2, 0)
-            step(row_max, i, 0)
-            step(leave, i - 3, 1, 0)
-            step(quant_u, i - 2, 1)
+            step(turn_bq, i + 4, 0)
+            step(quantize_u, i - 2, 1)
+            step(rank_1, i)
+            step(expo, i - 1, 1)
+            step(pack_bq, i + 4, 0)
+            step(turn_terms, i, 0)
+            step(turn_p, i - 1, 0)
+            step(dot, i + 2, 0)
             step(mix_aq, i + 1, 1)
-            step(quant_x, i + 3)
-            step(turn_x, i + 4, 1)
-            step(outs, i - 2, 0, 0)
+            step(row_max, i, 0)
+            step(leave, i - 2, 0, 1)
             step(recip, i - 1, 1)
-            step(expo, i, 0)
+            step(leave, i - 3, 1, 0)
             step(mix, i + 2, 0, 1, 1)
-            step(outs, i - 2, 1, 1)
-            step(weigh, i - 1, 0)
+            step(quantize_bq, i + 3)
             step(mix, i + 2, 0, 0, 0)
             step(norm, i - 1, 1)
+            step(expo, i, 0)
+            step(weigh, i - 1, 0)
+            step(turn_bq, i + 4, 1)
+            step(multiply_bv, i - 2, 0, 0)
             step(mix, i + 2, 0, 0, 1)
-            step(turn_mix, i + 1, 1)
-            step(row_max, i, 1)

import math
from contextlib import ExitStack

import concourse.mybir as mybir
from concourse.masks import make_identity

S, T, H, R, K = 4096, 256, 2, 2, 512
P = 128
PACK = 4
HALVES = 2
TILES = 2
UNIT = TILES * P
UNITS = S // UNIT
COLS = R * UNIT
ROW = R * K
AQ_UNITS = 2

FLOPS = 2 * 2 * (S * R) * (T * R) * K

F32 = mybir.dt.float32
BF16 = mybir.dt.bfloat16
U32 = mybir.dt.uint32
U8 = mybir.dt.uint8
FP8 = mybir.dt.float8_e4m3fn
FP8X4 = mybir.dt.float8_e4m3fn_x4
ALU = mybir.AluOpType
ACT = mybir.ActivationFunctionType
AXIS = mybir.AxisListType


def shared_on_gpsimd(u):
    return 3 <= u < UNITS - 4


def tile_tensorproductfactordecode_t_kernel(tc, bq_bytes, bq_scale, aq, bk, ak, av, bv, out):
    nc = tc.nc
    with ExitStack() as ctx:
        keep = ctx.enter_context(tc.tile_pool(name="keep", bufs=1))
        work = ctx.enter_context(tc.tile_pool(name="work", bufs=2))
        psum = ctx.enter_context(tc.psum_pool(name="psum", bufs=1))

        ident = keep.tile([P, P], F32, name="ident")
        make_identity(nc, ident[:])

        ctx.enter_context(tc.manual_schedule())

        def buf(tag, bufs, shape, dtype, align=64):
            return work.tile(shape, dtype, name=tag, tag=tag, bufs=bufs, align_bytes=align)

        def bank(tag, bufs, shape):
            return psum.tile(shape, F32, name=tag, tag=tag, bufs=bufs)

        bq_tiles = [keep.tile([P, TILES * ROW], U8, name=f"bq{u}", align_bytes=64) for u in range(UNITS)]
        scales = keep.tile([P, TILES * ROW], F32, name="scales")
        aq_cols = [keep.tile([P, AQ_UNITS * UNIT, H, R], BF16, name=f"aq_cols{c}") for c in range(UNITS // AQ_UNITS)]
        aq_raw = keep.tile([P, S // P, H * R], BF16, name="aq_raw")
        ak_raw = keep.tile([P, HALVES * H * R], BF16, name="ak_raw")
        av_raw = keep.tile([P, HALVES * H * R], BF16, name="av_raw")
        bk_raw = keep.tile([P, PACK, K], BF16, name="bk_raw", align_bytes=64)
        bv_raw = keep.tile([P, PACK, K], BF16, name="bv_raw", align_bytes=64)

        bq_view = bq_bytes.rearrange("(n p) r k -> p n (r k)", p=P)
        aq_flat = aq.rearrange("s h r -> (s h r)")

        def load_bq(u):
            nc.sync.dma_start(
                out=bq_tiles[u][:].rearrange("p (n c) -> p n c", n=TILES),
                in_=bq_view[:, TILES * u : TILES * (u + 1), :],
            )

        def load_aq(c):
            n = AQ_UNITS * UNIT * H * R
            nc.sync.dma_start(
                out=aq_cols[c][:].rearrange("p s h r -> p (s h r)"),
                in_=aq_flat[c * n : (c + 1) * n].partition_broadcast(P),
            )

        load_bq(0)
        nc.scalar.dma_start(out=scales[:, 0:K], in_=bq_scale.rearrange("a b k -> (a b k)").partition_broadcast(P))
        nc.sync.dma_start(out=bk_raw[:].rearrange("p x k -> p (x k)"), in_=bk.rearrange("(p a) j k -> p (a j k)", p=P))
        nc.scalar.dma_start(out=ak_raw[:], in_=ak.rearrange("(p a) h j -> p (a h j)", p=P))
        nc.scalar.dma_start(out=av_raw[:], in_=av.rearrange("(p a) h r -> p (a h r)", p=P))
        load_aq(0)
        load_bq(1)
        nc.sync.dma_start(out=aq_raw[:], in_=aq.rearrange("(n p) h r -> p n (h r)", p=P))
        nc.sync.dma_start(out=bv_raw[:].rearrange("p x k -> p (x k)"), in_=bv.rearrange("(p a) r k -> p (a r k)", p=P))
        for u in range(AQ_UNITS, UNITS):
            load_bq(u)
            if u % AQ_UNITS == 0:
                load_aq(u // AQ_UNITS)

        warm = keep.tile([P, 1], F32, name="warm")
        nc.vector.memset(warm[:], 0.0)
        warm_out = keep.tile([P, 1], F32, name="warm_out")
        nc.scalar.activation(warm_out[:], warm[:], ACT.Exp)

        nc.vector.tensor_copy(scales[:, K : 2 * K], scales[:, 0:K])
        nc.vector.tensor_copy(scales[:, 2 * K : 4 * K], scales[:, 0 : 2 * K])

        ak_neg = keep.tile([P, HALVES, H, R], F32, name="ak_neg")
        nc.gpsimd.tensor_scalar(
            ak_neg[:].rearrange("p a h j -> p (a h j)"), ak_raw[:], -1.0 / math.sqrt(K), 0.0, op0=ALU.mult, op1=ALU.add
        )
        av_f = keep.tile([P, H, HALVES, R], F32, name="av_f")
        nc.gpsimd.tensor_copy(av_f[:], av_raw[:].rearrange("p (a h r) -> p h a r", a=HALVES, h=H))
        aq_f = keep.tile([P, S // P, H, R], F32, name="aq_f")
        nc.gpsimd.tensor_copy(
            out=aq_f[:].rearrange("p n h r -> p (n h r)"), in_=aq_raw[:].rearrange("p n c -> p (n c)")
        )

        bk_codes = keep.tile([P, PACK * P], U32, name="bk_codes", align_bytes=64)
        bk_bytes = keep.tile([P, PACK * P], U8, name="bk_bytes", align_bytes=64)
        bv_codes = keep.tile([P, K], U32, name="bv_codes", align_bytes=64)
        bv_bytes = keep.tile([P, K], U8, name="bv_bytes", align_bytes=64)
        bk_packed = keep.tile([P, PACK * P * PACK], BF16, name="bk_packed", align_bytes=64)
        bv_packed = keep.tile([P, K, PACK], BF16, name="bv_packed", align_bytes=64)

        def transpose_words(dst, words, base):
            for w in range(2):
                nc.tensor.transpose(dst(w), words[:, base + w : base + K // 2 : 2], ident[:])

        def turn_bk():
            words = bk_raw[:].rearrange("p x k -> p (x k)").bitcast(F32)
            packed = bk_packed[:].bitcast(F32).rearrange("p (c w) -> p c w", w=2)
            for pair in range(2):
                turned = bank("o", 2, [P, 2, 2 * P])
                for x in range(2):
                    cols = slice(x * P, (x + 1) * P)
                    transpose_words(lambda w: turned[:, w, cols], words, (2 * pair + x) * (K // 2))
                nc.scalar.copy(
                    out=packed[:, pair * 2 * P : (pair + 1) * 2 * P, :], in_=turned[:].rearrange("p w c -> p c w")
                )

        def quantize_bk():
            nc.vector.quantize_mx(out=bk_codes[:].bitcast(FP8X4), scales=bk_bytes[:], in_=bk_packed[:])

        def pack_bv(quarter):
            n = slice(quarter * P, (quarter + 1) * P)
            nc.scalar.copy(out=bv_packed[:, n, :], in_=bv_raw[:, :, n].rearrange("p x n -> p n x"))

        def quantize_bv():
            nc.vector.quantize_mx(
                out=bv_codes[:].bitcast(FP8X4), scales=bv_bytes[:], in_=bv_packed[:].rearrange("p n x -> p (n x)")
            )

        live = {}

        def scale_bq(u):
            bq = buf("bq", 4, [P, TILES * ROW], BF16)
            nc.vector.tensor_tensor(out=bq[:], in0=bq_tiles[u][:].bitcast(FP8), in1=scales[:], op=ALU.mult)
            live["bq", u] = bq

        def turn_bq(u, tile):
            words = live["bq", u][:].bitcast(F32)
            turned = bank("bq_turned", 1, [P, 2, R * P])
            for r in range(R):
                cols = slice(r * P, (r + 1) * P)
                transpose_words(lambda w: turned[:, w, cols], words, (tile * R + r) * (K // 2))
            live["turned", u, tile] = turned

        def pack_bq(u, tile):
            if ("packed", u) not in live:
                live["packed", u] = buf("packed", 2, [P, COLS * PACK], BF16)
            packed = live["packed", u][:].bitcast(F32).rearrange("p (r n s w) -> p r n s w", r=R, n=TILES, w=2)
            nc.scalar.copy(
                packed[:, :, tile, :, :], live.pop(("turned", u, tile))[:].rearrange("p w (r s) -> p r s w", r=R)
            )

        def quantize_bq(u):
            codes = buf("codes", 2, [P, COLS], U32)
            scale_bytes = buf("scale_bytes", 2, [P, COLS], U8)
            nc.vector.quantize_mx(
                out=codes[:].bitcast(FP8X4), scales=scale_bytes[:], in_=live.pop(("packed", u))[:]
            )
            live["bq_mx", u] = (codes, scale_bytes)

        def dot(u, a):
            codes, scale_bytes = live["bq_mx", u]
            for j in range(R):
                dots = bank(f"dot{j}", 1, [P, COLS])
                cols = slice((2 * a + j) * P, (2 * a + j + 1) * P)
                nc.tensor.matmul_mx(
                    out=dots[:],
                    lhsT=bk_codes[:, cols].bitcast(FP8X4),
                    lhsT_scale=bk_bytes[:, cols],
                    rhs=codes[:].bitcast(FP8X4),
                    rhs_scale=scale_bytes[:],
                    start=True,
                    stop=True,
                )
                live["dot", u, a, j] = dots

        def aq_of_head_0(u):
            first = (u % AQ_UNITS) * UNIT
            return aq_cols[u // AQ_UNITS][:, first : first + UNIT, 0, :].rearrange("p c r -> p r c")

        def by_rank(tile_ap):
            return tile_ap.rearrange("p (r c) -> p r c", r=R)

        def mix(u, a, j, h):
            term = buf(f"term{h}", 8, [P, COLS], F32)
            dots = live["dot", u, a, j]
            factor = ak_neg[:, a, h, j : j + 1]
            if h == 0 and not (j == 0 and shared_on_gpsimd(u)):
                nc.vector.scalar_tensor_tensor(
                    out=by_rank(term[:]),
                    in0=by_rank(dots[:]),
                    scalar=factor,
                    in1=aq_of_head_0(u),
                    op0=ALU.mult,
                    op1=ALU.mult,
                )
            else:
                nc.scalar.activation(term[:], dots[:], ACT.Copy, scale=factor)
            live["term", u, a, j, h] = term

        def mix_aq(u, a):
            if not shared_on_gpsimd(u):
                return
            term = buf("term_aq", 6, [P, COLS], F32)
            nc.gpsimd.tensor_tensor(
                out=by_rank(term[:]), in0=by_rank(live["term", u, a, 0, 0][:]), in1=aq_of_head_0(u), op=ALU.mult
            )
            live["term", u, a, 0, 0] = term

        def turn_terms(u, h):
            groups = [range(R)] if h == 0 else [(r,) for r in range(R)]
            for g, ranks in enumerate(groups):
                scores = bank("scores", 2, [P, TILES, T])
                for tile in range(TILES):
                    for a in range(HALVES):
                        summed = [(j, r) for j in range(R) for r in ranks]
                        for n, (j, r) in enumerate(summed):
                            first = r * UNIT + tile * P
                            nc.tensor.matmul(
                                scores[:, tile, a * P : (a + 1) * P],
                                live["term", u, a, j, h][:, first : first + P],
                                ident[:],
                                start=(n == 0),
                                stop=(n == len(summed) - 1),
                                is_transpose=True,
                            )
                live["sum", u, h, g] = scores
            if h == 0:
                live["score", u, 0] = live["sum", u, 0, 0]

        def rank_0(u):
            part = buf("part", 3, [P, TILES, T], F32)
            summed = live.pop(("sum", u, 1, 0))
            for tile in range(TILES):
                nc.scalar.activation(
                    part[:, tile, :], summed[:, tile, :], ACT.Copy, scale=aq_f[:, TILES * u + tile, 1, 0:1]
                )
            live["part", u] = part

        def rank_1(u):
            score = buf("score", 3, [P, TILES, T], F32)
            summed = live.pop(("sum", u, 1, 1))
            part = live.pop(("part", u))
            for tile in range(TILES):
                nc.vector.scalar_tensor_tensor(
                    out=score[:, tile, :],
                    in0=summed[:, tile, :],
                    scalar=aq_f[:, TILES * u + tile, 1, 1:2],
                    in1=part[:, tile, :],
                    op0=ALU.mult,
                    op1=ALU.add,
                )
            live["score", u, 1] = score

        def row_max(u, h):
            lowest = buf("lowest", 4, [P, TILES], F32, 32)
            nc.vector.tensor_reduce(out=lowest[:], in_=live["score", u, h][:], axis=AXIS.X, op=ALU.min)
            live["lowest", u, h] = lowest

        def expo(u, h):
            e = buf("e", 4, [P, TILES, T], F32)
            total = buf("total", 4, [P, TILES], F32, 32)
            score = live.pop(("score", u, h))
            lowest = live.pop(("lowest", u, h))
            for tile in range(TILES):
                nc.scalar.activation(
                    e[:, tile, :],
                    score[:, tile, :],
                    ACT.Exp,
                    bias=lowest[:, tile : tile + 1],
                    scale=-1.0,
                    accum_out=total[:, tile : tile + 1],
                )
            live["e", u, h] = (e, total)

        def recip(u, h):
            inverse = buf("inverse", 4, [P, TILES], F32, 32)
            nc.vector.reciprocal(inverse[:], live["e", u, h][1][:])
            live["inverse", u, h] = inverse

        def norm(u, h):
            prob = buf("prob", 4, [P, TILES, T], F32)
            e = live.pop(("e", u, h))[0]
            inverse = live.pop(("inverse", u, h))
            for tile in range(TILES):
                by = inverse[:, tile : tile + 1]
                if u < UNITS - 1:
                    nc.gpsimd.tensor_scalar(prob[:, tile, :], e[:, tile, :], by, 0.0, op0=ALU.mult, op1=ALU.add)
                else:
                    nc.vector.tensor_scalar(prob[:, tile, :], e[:, tile, :], by, None, op0=ALU.mult)
            live["prob", u, h] = prob

        def turn_p(u, h):
            prob = live.pop(("prob", u, h))
            turned = bank("p_turned", 1, [P, HALVES, TILES, P])
            for tile in range(TILES):
                for a in range(HALVES):
                    nc.tensor.transpose(turned[:, a, tile, :], prob[:, tile, a * P : (a + 1) * P], ident[:])
            live["p_turned", u, h] = turned

        def weigh(u, h):
            weighted = buf("weighted", 3, [P, UNIT, HALVES, R], BF16)
            turned = live.pop(("p_turned", u, h))
            shape = [P, UNIT, HALVES, R]
            nc.vector.tensor_tensor(
                out=weighted[:],
                in0=turned[:].rearrange("p a n s -> p (n s) a").unsqueeze(3).to_broadcast(shape),
                in1=av_f[:, h].unsqueeze(1).to_broadcast(shape),
                op=ALU.mult,
            )
            live["weighted", u, h] = weighted

        def quantize_u(u, h):
            codes = buf("u_codes", 3, [P, UNIT], U32)
            scale_bytes = buf("u_bytes", 3, [P, UNIT], U8)
            nc.vector.quantize_mx(
                out=codes[:].bitcast(FP8X4),
                scales=scale_bytes[:],
                in_=live.pop(("weighted", u, h))[:].rearrange("p c a r -> p (c a r)"),
            )
            live["u_mx", u, h] = (codes, scale_bytes)

        def multiply_bv(u, h, tile):
            codes, scale_bytes = live["u_mx", u, h]
            result = bank("o", 2, [P, K])
            cols = slice(tile * P, (tile + 1) * P)
            nc.tensor.matmul_mx(
                out=result[:],
                lhsT=codes[:, cols].bitcast(FP8X4),
                lhsT_scale=scale_bytes[:, cols],
                rhs=bv_codes[:].bitcast(FP8X4),
                rhs_scale=bv_bytes[:],
                start=True,
                stop=True,
            )
            live["result", u, h, tile] = result

        out_view = out.rearrange("h (n p) k -> h p n k", p=P)

        def leave(u, h, tile):
            if ("stage", u, h) not in live:
                live["stage", u, h] = buf("stage", 5, [P, TILES, K], F32)
                live["left", u, h] = 0
            stage = live["stage", u, h]
            nc.scalar.copy(stage[:, tile, :], live.pop(("result", u, h, tile))[:])
            live["left", u, h] += 1
            if u == UNITS - 1:
                nc.sync.dma_start(out=out_view[h, :, TILES * u + tile, :], in_=stage[:, tile, :])
            elif live["left", u, h] == TILES:
                nc.sync.dma_start(out=out_view[h, :, TILES * u : TILES * (u + 1), :], in_=stage[:])

        def step(do, u, *rest):
            if 0 <= u < UNITS:
                do(u, *rest)

        turn_bk()
        for i in range(-5, UNITS + 3):
            if i == -2:
                quantize_bk()
            if i == 2:
                quantize_bv()
            if -3 <= i < 1:
                pack_bv(i + 3)
            step(leave, i - 3, 0, 0)
            step(multiply_bv, i - 3, 1, 1)
            step(row_max, i - 1, 1)
            step(turn_terms, i, 1)
            step(mix, i + 1, 0, 1, 0)
            step(pack_bq, i + 3, 1)
            step(leave, i - 3, 1, 1)
            step(turn_p, i - 2, 1)
            step(dot, i + 1, 1)
            step(quantize_u, i - 2, 0)
            step(recip, i - 1, 0)
            step(multiply_bv, i - 2, 0, 1)
            step(scale_bq, i + 5)
            step(mix, i + 1, 1, 0, 0)
            step(rank_0, i)
            step(weigh, i - 2, 1)
            step(mix, i + 1, 1, 1, 1)
            step(multiply_bv, i - 3, 1, 0)
            step(mix_aq, i, 0)
            step(mix, i + 1, 1, 0, 1)
            step(norm, i - 1, 0)
            step(mix, i + 1, 1, 1, 0)
            step(turn_bq, i + 4, 0)
            step(quantize_u, i - 2, 1)
            step(rank_1, i)
            step(expo, i - 1, 1)
            step(pack_bq, i + 4, 0)
            step(turn_terms, i, 0)
            step(turn_p, i - 1, 0)
            step(dot, i + 2, 0)
            step(mix_aq, i + 1, 1)
            step(row_max, i, 0)
            step(leave, i - 2, 0, 1)
            step(recip, i - 1, 1)
            step(leave, i - 3, 1, 0)
            step(mix, i + 2, 0, 1, 1)
            step(quantize_bq, i + 3)
            step(mix, i + 2, 0, 0, 0)
            step(norm, i - 1, 1)
            step(expo, i, 0)
            step(weigh, i - 1, 0)
            step(turn_bq, i + 4, 1)
            step(multiply_bv, i - 2, 0, 0)
            step(mix, i + 2, 0, 0, 1)
